import numpy as np, ml_dtypes
CORES = [16,32,48,64,80]
N = 5
import mx_ref
BF = ml_dtypes.bfloat16
def entries(a):
    return np.ascontiguousarray(a.T).reshape(-1)
def table(e):
    return np.ascontiguousarray(np.reshape(e, (-1, 16)).T).astype(np.int32)
def cols(t, e):
    v = np.concatenate([t.reshape(128, -1, 4), np.zeros((128, 1, 4), BF)], axis=1)
    return np.ascontiguousarray(v[:, e]).reshape(128, -1)
def cut(t, i, w=512):
    return t[:, w * i:w * i + w]
def f(rng, *shape):
    return mx_ref.flush((rng.standard_normal(shape, dtype=np.float32) * np.exp2(rng.integers(-2, 3, shape[:-1] + (1,)))).astype(BF))
def wide(rng, *shape, cols=0):
    v = rng.standard_normal(shape, dtype=np.float32) * np.exp2(rng.integers(-12, 13, shape)).astype(np.float32)
    if cols: v *= np.repeat(np.exp2(rng.integers(-cols, cols + 1, shape[:-2] + (1, shape[-1] // 4))) * (rng.random(shape[:-2] + (1, shape[-1] // 4)) > 0.0625), 4, axis=-1).astype(np.float32)
    return mx_ref.flush(v.astype(BF))
TB, T, CAPP, O = 512, 384, 64, 2
def lists(rng, case=""):
    o = []; odd = rng.permutation(N)
    for r in range(N):
        lo, hi = {"one": (1, 1), "full": (CAPP, CAPP), "runs": (1, CAPP // 2), "none": (1, CAPP)}.get(case, (0, CAPP))
        n = rng.integers(lo, hi + 1, N)
        if case == "none":
            if r == odd[0]: n[:] = 0; n[rng.integers(0, N)] = 1
            elif r == odd[1]: n[r] = 0
            elif r == odd[2]: n[np.arange(N) != r] = 0
            else: n[rng.permutation(N)[:rng.integers(1, N)]] = 0
        if n.sum() == 0: n[rng.integers(0, N)] = 1
        if case == "full": named = [np.append([0, TB - 1], 1 + rng.permutation(TB - 2)[:n[q] - 2]) for q in range(N)]
        else: named = [rng.permutation(TB)[:n[q]] for q in range(N)]
        pool = rng.permutation(np.concatenate([q * TB + named[q] for q in range(N)]))
        i = np.arange(len(pool))
        k = T - len(pool)
        i = np.concatenate([i, (rng.random(k) * rng.random(k) * len(pool)).astype(int)])
        i = np.sort(i) if case == "runs" else rng.permutation(i)
        o.append(table(pool[i]))
    return {"want": np.stack(o)}
def setup_inputs(rng):
    return {"x": f(rng, N, 128, 4 * TB), "w": f(rng, N, 128, 512 * O), **lists(rng)}
def setup_inputs_one(rng):
    return {**setup_inputs(rng), **lists(rng, "one")}
def setup_inputs_full(rng):
    return {**setup_inputs(rng), **lists(rng, "full")}
def setup_inputs_runs(rng):
    return {**setup_inputs(rng), **lists(rng, "runs")}
def setup_inputs_none(rng):
    return {**setup_inputs(rng), **lists(rng, "none")}
def setup_inputs_spread(rng):
    d = setup_inputs(rng); d["x"] = wide(rng, N, 128, 4 * TB, cols=8); return d
def check_inputs(d):
    b = []
    for r in range(N):
        e = entries(d["want"][r])
        if e.min() < 0 or e.max() >= N * TB or any(len(np.unique(e[e // TB == q])) > CAPP for q in range(N)): b.append("want")
    return b
def reference(x, w, want):
    every = np.concatenate([x[q] for q in range(N)], axis=1)
    y = np.zeros((N, 128, O * T), np.float32)
    for r in range(N):
        t = mx_ref.quantize(cols(every, entries(want[r])))
        for o in range(O):
            y[r][:, T * o:T * o + T] = mx_ref.matmul(mx_ref.quantize(np.ascontiguousarray(cut(w[r], o))), t)
    return {"y": y}

@@ -1,0 +1,246 @@
+import numpy as np
+from concourse.bass import DstId, RemoteDMATransfer
+from concourse.mybir import dt, AluOpType, AxisListType, ActivationFunctionType
+
+N, TB, NT, CAPP, O = 5, 512, 384, 64, 2
+P = 4
+F32, BF, U16, I32 = "float32", "bfloat16", "uint16", "int32"
+SCRATCH = {
+    "tabi": ("sbuf", [128, 24], I32), "tabp": ("sbuf", [128, 32], F32), "jt": ("sbuf", [128, 32], F32),
+    "offk": ("sbuf", [128, 24], U16), "lutk": ("sbuf", [128, 2560], F32), "ii": ("sbuf", [128, 384], F32),
+    "kk": ("sbuf", [128, 384], F32), "nb": ("sbuf", [128, 4], F32),
+    "ab0": ("sbuf", [128, 384], F32), "ab1": ("sbuf", [128, 384], F32), "ab2": ("sbuf", [128, 384], F32),
+    "ab3": ("sbuf", [128, 384], F32),
+    "rr": ("sbuf", [128, 4], F32), "yy": ("sbuf", [128, 32], F32), "ft": ("sbuf", [128, 32], F32),
+    "iw": ("sbuf", [128, 528], F32), "zero": ("sbuf", [128, 384], F32),
+    "pci": ("sbuf", [128, 1], I32), "pbi": ("sbuf", [128, 3], I32), "pf": ("sbuf", [128, 3], F32), "par0": ("sbuf", [128, 1], F32),
+    "nq": ("sbuf", [128, 1], F32), "a64": ("sbuf", [128, 1], F32),
+    "i16": ("sbuf", [128, 24], F32), "idx": ("sbuf", [128, 24], F32), "ih0": ("sbuf", [128, 12], F32), "ih": ("sbuf", [128, 12], F32),
+    "cr0": ("sbuf", [128, 8], F32), "cr": ("sbuf", [128, 8], U16),
+    "e1": ("sbuf", [128, 24], F32), "a1": ("sbuf", [128, 24], F32), "bb": ("sbuf", [128, 24], F32), "el": ("sbuf", [128, 24], F32),
+    "g1": ("sbuf", [128, 24], F32), "s1": ("sbuf", [128, 24], F32), "off": ("sbuf", [128, 24], U16),
+    "h0": ("sbuf", [128, 12], F32), "h1": ("sbuf", [128, 12], F32), "hs": ("sbuf", [128, 12], F32), "hn": ("sbuf", [128, 12], F32),
+    "vt": ("sbuf", [128, 12], F32), "hoff": ("sbuf", [128, 12], U16), "ev": ("sbuf", [128, 192], F32),
+    "ind": ("sbuf", [128, 384], F32), "ss": ("sbuf", [128, 384], F32), "st": ("sbuf", [128, 384], F32),
+    "zf": ("sbuf", [128, 12], F32), "zo": ("sbuf", [128, 12], U16), "cw": ("sbuf", [128, 448], F32),
+    "dd": ("sbuf", [128, 128], F32), "dtr": ("sbuf", [128, 128], F32), "lq": ("sbuf", [128, 4], F32), "ls": ("sbuf", [128, 16], F32),
+    "lin": ("sbuf", [128, 16], F32), "offx": ("sbuf", [128, 64], U16),
+    "xs": ("sbuf", [128, 2048], BF), "ws": ("sbuf", [128, 1024], BF), "hx": ("sbuf", [128, 1024], BF), "ho": ("sbuf", [128, 1536], BF),
+    "qw": ("sbuf", [128, 256], "float8_e4m3fn_x4"), "sw": ("sbuf", [128, 256], "uint8"),
+    "qx": ("sbuf", [128, 256], "float8_e4m3fn_x4"), "sx": ("sbuf", [128, 256], "uint8"),
+    "qo": ("sbuf", [128, 384], "float8_e4m3fn_x4"), "so": ("sbuf", [128, 384], "uint8"),
+    "qr": ("sbuf", [128, 256], "float8_e4m3fn_x4"), "sr": ("sbuf", [128, 256], "uint8"),
+    "fd": ("sbuf", [128, 48], U16), "sg": ("sbuf", [128, 768], F32), "sgt": ("sbuf", [128, 768], F32),
+    "nbb": ("sbuf", [128, 24], F32), "q0": ("sbuf", [128, 24], F32), "q1": ("sbuf", [128, 24], F32), "qa": ("sbuf", [128, 24], F32),
+    "q2": ("sbuf", [128, 24], F32), "qb": ("sbuf", [128, 24], F32), "q3": ("sbuf", [128, 24], F32),
+    "oe": ("sbuf", [128, 24], F32), "oa": ("sbuf", [128, 24], F32), "om": ("sbuf", [128, 24], F32), "oi": ("sbuf", [128, 24], F32),
+    "ov": ("sbuf", [128, 24], F32), "q4": ("sbuf", [128, 24], F32), "yoff": ("sbuf", [128, 24], U16),
+    "oc": ("sbuf", [128, 24], F32), "od": ("sbuf", [128, 24], F32), "offo": ("sbuf", [128, 96], U16),
+    "py0": ("sbuf", [128, 640], F32), "py1": ("sbuf", [128, 640], F32), "yo": ("sbuf", [128, 768], F32),
+    "pso": ("psum", [128, 1024], F32), "psr": ("psum", [128, 1024], F32),
+}
+SEMAPHORES = ["cv", "cs", "cg", "ct", "dw", "dx", "dwt", "dy", "lloc", "larr", "cloc", "carr"]
+
+
+def rank_program(g, core, T, topo):
+    r = T.rank_of(core)
+    if r is None:
+        return
+    A, AF, X = AluOpType, ActivationFunctionType, AxisListType.X
+    peers = [(r + 1 + a) % N for a in range(P)]
+    eng = {"v": g.vector, "s": g.scalar, "g": g, "t": g.tensor, "y": g.sync}
+    cnt = {"v": 0, "s": 0, "g": 0, "t": 0}
+    seen = {q: {} for q in eng}
+
+    def need(q, deps):
+        for d in deps:
+            if isinstance(d, list):
+                need(q, d)
+                continue
+            sem, val = d
+            if seen[q].get(sem, 0) < val:
+                eng[q].wait_ge(T.sem[sem], val)
+                seen[q][sem] = val
+
+    def op(q, deps, fn, *args, **kw):
+        need(q, deps)
+        cnt[q] += 1
+        fn(*args, **kw).then_inc(T.sem["c" + q], 1)
+        return ("c" + q, cnt[q])
+
+    V, S, G, M = g.vector, g.scalar, g, g.tensor
+
+    for i in range(8):
+        (g.sync if i % 2 == 0 else g.scalar).dma_start(T.tabi[16 * i:16 * i + 16, 0:24], T.want[:, :]).then_inc(T.sem.dw, 16)
+    DW, DX, DWT = ("dw", 128), ("dx", 16), ("dwt", 16)
+    g.sync.dma_start(T.xs[:, :], T.x[:, :]).then_inc(T.sem.dx, 16)
+    g.sync.dma_start(T.ws[:, :], T.w[:, :]).then_inc(T.sem.dwt, 16)
+
+    L0 = op("g", [], G.iota, T.lutk[:, 0:256], [[1024, 256]], 0, 0, allow_small_or_imprecise_dtypes=True)
+    L1 = op("g", [], G.iota, T.lutk[:, 256:512], [[1024, 256]], 262144, 0, allow_small_or_imprecise_dtypes=True)
+    II = op("g", [], G.iota, T.ii[:, :], [[1, 384]], 0, 0, allow_small_or_imprecise_dtypes=True)
+    PC = op("g", [], G.iota, T.pci[:, :], [[0, 1]], 0, 1)
+    I16 = op("g", [], G.iota, T.i16[:, :], [[16, 24]], 0, 0, allow_small_or_imprecise_dtypes=True)
+    IH0 = op("g", [], G.iota, T.ih0[:, :], [[32, 12]], CAPP, 0, allow_small_or_imprecise_dtypes=True)
+    CR0 = op("g", [], G.iota, T.cr0[:, :], [[16, 4], [0, 2]], 0, 0, allow_small_or_imprecise_dtypes=True)
+    TP0 = op("v", [], V.memset, T.tabp[:, 24:32], 0.0)
+    NQ = [op("v", [], V.memset, T.nq[32 * a:32 * a + 32, :], float(-peers[a])) for a in range(P)]
+    lk = [L0, L1]
+    for k in range(2, 6):
+        lk.append(op("v", [L0], V.tensor_scalar, T.lutk[:, 256 * k:256 * k + 256], T.lutk[:, 0:256], 262144.0 * k, None, A.add))
+    for k in range(6, 10):
+        lk.append(op("s", [L0], S.activation, T.lutk[:, 256 * k:256 * k + 256], T.lutk[:, 0:256], AF.Identity, bias=262144.0 * k))
+    ZR = op("s", [L1], S.activation, T.zero[:, :], T.lutk[:, 0:384], AF.Copy, scale=0.0)
+    IW = [op("v", [], V.memset, T.iw[:, 0:512], 1.0), op("v", [], V.memset, T.iw[:, 512:528], 0.0)]
+    CW0 = op("v", [], V.memset, T.cw[:, 0:CAPP], 0.0)
+
+    OK = op("v", [DW], V.tensor_copy, T.offk[:, :], T.tabi[:, :])
+    TP = op("v", [], V.tensor_copy, T.tabp[:, 0:24], T.tabi[:, :])
+    JT = op("v", [TP, TP0], V.transpose, T.jt[:, :], T.tabp[:, :])
+    KK = op("v", [OK, II, lk], V.tensor_tensor, T.kk[:, :], T.lutk[:, 0:2560].indirect(T.offk[:, 0:24]), T.ii[:, :], A.add)
+    NB = [op("s", [JT], S.activation, T.nb[32 * a:32 * a + 32, :], T.jt[32 * a:32 * a + 32, 4 * a:4 * a + 4], AF.Copy, scale=-1024.0)
+          for a in range(P)]
+    PB = [op("v", [PC], V.tensor_scalar, T.pbi[:, 0:1], T.pci[:, :], 15, None, A.bitwise_and),
+          op("v", [], V.tensor_scalar, T.pbi[:, 1:2], T.pci[:, :], 31, None, A.bitwise_and),
+          op("v", [], V.tensor_scalar, T.pbi[:, 2:3], T.pci[:, :], 4, 1, A.arith_shift_right, A.bitwise_and)]
+    E1 = op("v", [TP, NQ], V.tensor_scalar, T.e1[:, :], T.tabp[:, 0:24], 1.0 / 512, T.nq[:, 0:1], A.mult, A.add)
+    PF = op("v", [PB], V.tensor_copy, T.pf[:, :], T.pbi[:, :])
+    AB = [op("s", [NB, KK], S.activation, T.ab0[:, :], T.kk[:, :], AF.Abs, bias=T.nb[:, 0:1])]
+    A1 = op("s", [E1], S.activation, T.a1[:, :], T.e1[:, :], AF.Abs, bias=T.zero[:, 0:1]) if False else None
+    E1C = op("v", [E1], V.tensor_scalar, T.bb[:, :], T.e1[:, :], 255.5 / 512, None, A.subtract)
+    IDX = op("v", [PF, I16], V.tensor_scalar, T.idx[:, :], T.i16[:, :], T.pf[:, 0:1], None, A.add)
+    A1 = op("s", [E1C], S.activation, T.a1[:, :], T.bb[:, :], AF.Abs)
+    for k in range(1, 4):
+        AB.append(op("s", [], S.activation, T["ab%d" % k][:, :], T.kk[:, :], AF.Abs, bias=T.nb[:, k:k + 1]))
+    RR = [op("v", [AB[0]], V.tensor_reduce, T.rr[:, 0:1], T.ab0[:, :], X, A.min)]
+    BB = op("v", [A1], V.tensor_scalar, T.nbb[:, :], T.a1[:, :], 0.5, None, A.is_lt)
+    BO = op("v", [A1], V.tensor_scalar, T.bb[:, :], T.a1[:, :], 0.5, None, A.is_gt)
+    RR.append(op("v", [AB[1]], V.tensor_reduce, T.rr[:, 1:2], T.ab1[:, :], X, A.min))
+    EL = op("v", [BO, E1], V.tensor_tensor, T.el[:, :], T.bb[:, :], T.e1[:, :], A.max)
+    for k in range(2, 4):
+        RR.append(op("v", [AB[k]], V.tensor_reduce, T.rr[:, k:k + 1], T["ab%d" % k][:, :], X, A.min))
+    YY = []
+    for d in range(P):
+        for a in range(P):
+            o_, i_ = T.yy[32 * d:32 * d + 32, 4 * a:4 * a + 4], T.rr[32 * a:32 * a + 32, 0:4]
+            if d % 2 == 0:
+                YY.append(op("v", [RR], V.tensor_copy, o_, i_))
+            else:
+                YY.append(op("s", [RR], S.activation, o_, i_, AF.Copy))
+    YD = op("v", [YY], V.tensor_copy, T.yy[:, 16:32], T.yy[:, 0:16])
+    FT = op("v", [YD], V.transpose, T.ft[:, :], T.yy[:, :])
+    G1 = op("v", [FT, IDX], V.tensor_tensor, T.g1[:, :], T.idx[:, :], T.ft[:, 0:24], A.subtract)
+    S1 = op("v", [G1, EL], V.tensor_tensor, T.s1[:, :], T.g1[:, :], T.el[:, :], A.max)
+    OF = op("v", [S1], V.tensor_scalar, T.off[:, :], T.s1[:, :], 512.0, 512.0, A.mult, A.min)
+    IN = op("s", [OF, IW], S.activation, T.ind[:, :], T.iw[:, 0:528].indirect(T.off[:, 0:24]), AF.Copy)
+    P0 = op("v", [PF], V.tensor_scalar, T.par0[:, :], T.pf[:, 2:3], -1.0, 1.0, A.mult, A.add)
+    H1 = op("v", [S1], V.tensor_scalar, T.h1[:, :], T.s1[:, 1:24:2], T.pf[:, 2:3], None, A.mult)
+    H0 = op("v", [P0], V.tensor_scalar, T.h0[:, :], T.s1[:, 0:24:2], T.par0[:, 0:1], None, A.mult)
+    HS = op("v", [H0, H1], V.tensor_tensor, T.hs[:, :], T.h0[:, :], T.h1[:, :], A.add)
+    HO = op("v", [HS], V.tensor_scalar, T.hoff[:, :], T.hs[:, :], 512.0, 512.0, A.mult, A.min)
+    EV = op("s", [HO, lk], S.activation, T.ev[:, :], T.lutk[:, 0:528].indirect(T.hoff[:, 0:12]), AF.Copy)
+    HN = op("v", [HS], V.tensor_scalar, T.hn[:, :], T.hs[:, :], 1.0, None, A.is_ge)
+    IH = op("v", [IH0, PF], V.tensor_scalar, T.ih[:, :], T.ih0[:, :], T.pf[:, 1:2], None, A.add)
+    VT = op("v", [HN, IH], V.tensor_tensor, T.vt[:, :], T.hn[:, :], T.ih[:, :], A.mult)
+    CR = op("v", [CR0, PF], V.tensor_scalar, T.cr[:, :], T.cr0[:, :], T.pf[:, 0:1], None, A.add)
+    SS = op("v", [IN, ZR], V.tensor_tensor_scan, T.ss[:, :], T.ind[:, :], T.zero[:, :], -1.0, A.add, A.add)
+    ST = op("v", [SS], V.transpose, T.st[:, :], T.ss[:, :])
+    ZF = op("v", [ST, VT], V.tensor_tensor, T.zf[:, :], T.st[:, 0:384:32], T.vt[:, :], A.max)
+    ZO = op("v", [ZF], V.tensor_copy, T.zo[:, :], T.zf[:, :])
+    CW = op("v", [ZO, EV, CW0], V.tensor_copy, T.cw[:, 0:448].indirect(T.zo[:, 0:12]), T.ev[:, :])
+    DD = op("v", [CW, CR], V.tensor_copy, T.dd[:, :], T.cw[:, 0:CAPP].indirect(T.cr[:, 0:8]))
+    DT = op("v", [DD], V.transpose, T.dtr[:, :], T.dd[:, :])
+    LQ = op("v", [DT], V.tensor_tensor, T.lq[:, :], T.dtr[:, 0:128:32], T.dtr[:, 16:128:32], A.add)
+    LS = []
+    for d in range(P):
+        for a in range(P):
+            o_, i_ = T.ls[32 * d:32 * d + 32, 4 * a:4 * a + 4], T.lq[32 * a:32 * a + 32, 0:4]
+            if d % 2 == 0:
+                LS.append(op("v", [LQ], V.tensor_copy, o_, i_))
+            else:
+                LS.append(op("s", [LQ], S.activation, o_, i_, AF.Copy))
+    need("g", [LS])
+
+    def send(items, local):
+        tr = []
+        for a, (src, dst, sem) in items:
+            c = T.cores[peers[a]]
+            rid, pid, _ = topo.addr(c)
+            es = topo.engines(core, c)
+            n = len(es) // P
+            m = 0
+            for e in es[a * n:a * n + n]:
+                m |= 1 << e
+            tr.append(RemoteDMATransfer(dst_ids=[DstId(rid=rid, pnc=pid)], dma_engine_mask=m, remote_sem=sem, src=src, dst=dst))
+        g.remote_dma_fused(tr, local_sem=local)
+
+    back = [(r - peers[a] - 1) % N for a in range(P)]
+    ne = len(topo.engines(core, T.cores[peers[0]])) // P
+    send([(a, (T.ls[:, 4 * a:4 * a + 4], T.lin[:, 4 * back[a]:4 * back[a] + 4], T.sem.larr)) for a in range(P)], T.sem.lloc)
+
+    QW = op("v", [DWT], V.quantize_mx, T.qw[:, :], T.sw[:, :], T.ws[:, :])
+    FD = [op("v", [FT], V.tensor_copy, T.fd[:, 0:48:2], T.ft[:, 0:24]), op("v", [], V.tensor_copy, T.fd[:, 1:48:2], T.ft[:, 0:24])]
+    SG = op("s", [FD, SS], S.activation, T.sg[:, :], T.ss[:, 0:384].indirect(T.fd[:, 0:48]), AF.Copy)
+    A64 = [op("v", [], V.memset, T.a64[32 * a:32 * a + 32, :], float(CAPP * a)) for a in range(P)]
+    OC = op("v", [TP], V.tensor_scalar, T.oc[:, :], T.tabp[:, 0:24], 4.0, float(-4 * TB * r), A.mult, A.add)
+    OD = op("v", [OC], V.tensor_scalar, T.od[:, :], T.oc[:, :], 0.0, float(4 * TB - 4), A.max, A.min)
+    OO = [op("v", [OD], V.tensor_scalar, T.offo[:, 24 * t:24 * t + 24], T.od[:, :], float(t), None, A.add) for t in range(4)]
+
+    LA = ("larr", P * ne)
+    OX = [op("v", [LA], V.tensor_scalar, T.offx[:, 16 * t:16 * t + 16], T.lin[:, :], 1.0 / 256, float(t), A.mult, A.add) for t in range(4)]
+    HX = []
+    for t in range(4):
+        o_, i_ = T.hx[:, t:1024:4], T.xs[:, 0:2048].indirect(T.offx[:, 16 * t:16 * t + 16])
+        if t < 2:
+            HX.append(op("v", [OX[t], DX], V.tensor_copy, o_, i_))
+        else:
+            HX.append(op("s", [OX[t], DX], S.activation, o_, i_, AF.Copy))
+    QX = op("v", [HX], V.quantize_mx, T.qx[:, :], T.sx[:, :], T.hx[:, :])
+    need("g", [QX])
+    send([(a, (T.qx[:, 64 * a:64 * a + 64].bitcast(dt.uint8), T.qr[:, 64 * back[a]:64 * back[a] + 64].bitcast(dt.uint8), T.sem.carr))
+          for a in range(P)], T.sem.cloc)
+    send([(a, (T.sx[:, 64 * a:64 * a + 64], T.sr[:, 64 * back[a]:64 * back[a] + 64], T.sem.carr)) for a in range(P)], T.sem.cloc)
+
+    HO_ = []
+    for t in range(4):
+        o_, i_ = T.ho[:, t:1536:4], T.xs[:, 0:2048].indirect(T.offo[:, 24 * t:24 * t + 24])
+        if t < 2:
+            HO_.append(op("v", [OO[t]], V.tensor_copy, o_, i_))
+        else:
+            HO_.append(op("s", [OO[t]], S.activation, o_, i_, AF.Copy))
+    QO = op("v", [HO_], V.quantize_mx, T.qo[:, :], T.so[:, :], T.ho[:, :])
+    MO = [op("t", [QO, QW], M.matmul_mx, T.pso[:, 512 * o:512 * o + 384], T.qw[:, 128 * o:128 * o + 128], T.sw[:, 128 * o:128 * o + 128],
+             T.qo[:, :], T.so[:, :], True, True) for o in range(O)]
+    SGT = op("v", [SG], V.transpose, T.sgt[:, :], T.sg[:, :])
+    Q0 = op("v", [SGT, A64], V.tensor_scalar, T.q0[:, :], T.sgt[:, 0:768:32], T.a64[:, 0:1], None, A.add)
+    Q1 = op("v", [Q0, BB], V.tensor_tensor, T.q1[:, :], T.q0[:, :], T.nbb[:, :], A.mult)
+    QA = [op("v", [Q1], V.tensor_copy, T.qa[64 * h:64 * h + 64, :], T.q1[64 - 64 * h:128 - 64 * h, :]) for h in range(2)]
+    OE = op("v", [TP], V.tensor_scalar, T.oe[:, :], T.tabp[:, 0:24], float(TB * r), None, A.is_ge)
+    OA = op("v", [TP], V.tensor_scalar, T.oa[:, :], T.tabp[:, 0:24], float(TB * r + TB), None, A.is_lt)
+    Q2 = op("v", [QA, Q1], V.tensor_tensor, T.q2[:, :], T.q1[:, :], T.qa[:, :], A.add)
+    OM = op("v", [OE, OA], V.tensor_tensor, T.om[:, :], T.oe[:, :], T.oa[:, :], A.mult)
+    QB = [op("v", [Q2], V.tensor_copy, T.qb[32 * a:32 * a + 32, :], T.q2[32 * (a ^ 1):32 * (a ^ 1) + 32, :]) for a in range(P)]
+    OI = op("v", [IDX], V.tensor_scalar, T.oi[:, :], T.idx[:, :], float(CAPP * P), None, A.add)
+    Q3 = op("v", [QB, Q2], V.tensor_tensor, T.q3[:, :], T.q2[:, :], T.qb[:, :], A.add)
+    OV = op("v", [OM, OI], V.tensor_tensor, T.ov[:, :], T.om[:, :], T.oi[:, :], A.mult)
+    Q4 = op("v", [Q3, OV], V.tensor_tensor, T.q4[:, :], T.q3[:, :], T.ov[:, :], A.add)
+    YO = op("v", [Q4], V.tensor_copy, T.yoff[:, :], T.q4[:, :])
+    PO = [op("v", [MO[0]], V.tensor_copy, T.py0[:, 256:640], T.pso[:, 0:384]),
+          op("s", [MO[1]], S.activation, T.py1[:, 256:640], T.pso[:, 512:896], AF.Copy)]
+
+    CA = ("carr", 2 * P * ne)
+    MR = [op("t", [CA, QW], M.matmul_mx, T.psr[:, 512 * o:512 * o + 256], T.qw[:, 128 * o:128 * o + 128], T.sw[:, 128 * o:128 * o + 128],
+             T.qr[:, :], T.sr[:, :], True, True) for o in range(O)]
+    PR = [op("v", [MR[0]], V.tensor_copy, T.py0[:, 0:256], T.psr[:, 0:256]),
+          op("s", [MR[1]], S.activation, T.py1[:, 0:256], T.psr[:, 512:768], AF.Copy)]
+    nd = 0
+    for h in range(2):
+        c = 192 * h
+        Y0 = op("v", [PR[0], PO[0], YO], V.tensor_copy, T.yo[:, c:c + 192], T.py0[:, 0:640].indirect(T.yoff[:, 12 * h:12 * h + 12]))
+        Y1 = op("s", [PR[1], PO[1], YO], S.activation, T.yo[:, 384 + c:384 + c + 192], T.py1[:, 0:640].indirect(T.yoff[:, 12 * h:12 * h + 12]), AF.Copy)
+        for o, tok in ((0, Y0), (1, Y1)):
+            need("y", [tok])
+            g.sync.dma_start(T.y[:, 384 * o + c:384 * o + c + 192], T.yo[:, 384 * o + c:384 * o + c + 192]).then_inc(T.sem.dy, 16)
+            nd += 16
+    need("y", [("dy", nd)])
+    need("g", [("lloc", P * ne), ("cloc", 2 * P * ne)] + [("c" + q, cnt[q]) for q in cnt])

@@ -4,41 +4,24 @@ from concourse.mybir import dt, AluOpType, AxisListType, ActivationFunctionType
 
 N, TB, NT, CAPP, O = 5, 512, 384, 64, 2
 P = 4
-F32, BF, U16, I32 = "float32", "bfloat16", "uint16", "int32"
-SCRATCH = {
-    "tabi": ("sbuf", [128, 24], I32), "tabp": ("sbuf", [128, 32], F32), "jt": ("sbuf", [128, 32], F32),
-    "offk": ("sbuf", [128, 24], U16), "lutk": ("sbuf", [128, 2560], F32), "ii": ("sbuf", [128, 384], F32),
-    "kk": ("sbuf", [128, 384], F32), "nb": ("sbuf", [128, 4], F32),
-    "ab0": ("sbuf", [128, 384], F32), "ab1": ("sbuf", [128, 384], F32), "ab2": ("sbuf", [128, 384], F32),
-    "ab3": ("sbuf", [128, 384], F32),
-    "rr": ("sbuf", [128, 4], F32), "yy": ("sbuf", [128, 32], F32), "ft": ("sbuf", [128, 32], F32),
-    "iw": ("sbuf", [128, 528], F32), "zero": ("sbuf", [128, 384], F32),
-    "pci": ("sbuf", [128, 1], I32), "pbi": ("sbuf", [128, 3], I32), "pf": ("sbuf", [128, 3], F32), "par0": ("sbuf", [128, 1], F32),
-    "nq": ("sbuf", [128, 1], F32), "a64": ("sbuf", [128, 1], F32),
-    "i16": ("sbuf", [128, 24], F32), "idx": ("sbuf", [128, 24], F32), "ih0": ("sbuf", [128, 12], F32), "ih": ("sbuf", [128, 12], F32),
-    "cr0": ("sbuf", [128, 8], F32), "cr": ("sbuf", [128, 8], U16),
-    "e1": ("sbuf", [128, 24], F32), "a1": ("sbuf", [128, 24], F32), "bb": ("sbuf", [128, 24], F32), "el": ("sbuf", [128, 24], F32),
-    "g1": ("sbuf", [128, 24], F32), "s1": ("sbuf", [128, 24], F32), "off": ("sbuf", [128, 24], U16),
-    "h0": ("sbuf", [128, 12], F32), "h1": ("sbuf", [128, 12], F32), "hs": ("sbuf", [128, 12], F32), "hn": ("sbuf", [128, 12], F32),
-    "vt": ("sbuf", [128, 12], F32), "hoff": ("sbuf", [128, 12], U16), "ev": ("sbuf", [128, 192], F32),
-    "ind": ("sbuf", [128, 384], F32), "ss": ("sbuf", [128, 384], F32), "st": ("sbuf", [128, 384], F32),
-    "zf": ("sbuf", [128, 12], F32), "zo": ("sbuf", [128, 12], U16), "cw": ("sbuf", [128, 448], F32),
-    "dd": ("sbuf", [128, 128], F32), "dtr": ("sbuf", [128, 128], F32), "lq": ("sbuf", [128, 4], F32), "ls": ("sbuf", [128, 16], F32),
-    "lin": ("sbuf", [128, 16], F32), "offx": ("sbuf", [128, 64], U16),
-    "xs": ("sbuf", [128, 2048], BF), "ws": ("sbuf", [128, 1024], BF), "hx": ("sbuf", [128, 1024], BF), "ho": ("sbuf", [128, 1536], BF),
-    "qw": ("sbuf", [128, 256], "float8_e4m3fn_x4"), "sw": ("sbuf", [128, 256], "uint8"),
-    "qx": ("sbuf", [128, 256], "float8_e4m3fn_x4"), "sx": ("sbuf", [128, 256], "uint8"),
-    "qo": ("sbuf", [128, 384], "float8_e4m3fn_x4"), "so": ("sbuf", [128, 384], "uint8"),
-    "qr": ("sbuf", [128, 256], "float8_e4m3fn_x4"), "sr": ("sbuf", [128, 256], "uint8"),
-    "fd": ("sbuf", [128, 48], U16), "sg": ("sbuf", [128, 768], F32), "sgt": ("sbuf", [128, 768], F32),
-    "nbb": ("sbuf", [128, 24], F32), "q0": ("sbuf", [128, 24], F32), "q1": ("sbuf", [128, 24], F32), "qa": ("sbuf", [128, 24], F32),
-    "q2": ("sbuf", [128, 24], F32), "qb": ("sbuf", [128, 24], F32), "q3": ("sbuf", [128, 24], F32),
-    "oe": ("sbuf", [128, 24], F32), "oa": ("sbuf", [128, 24], F32), "om": ("sbuf", [128, 24], F32), "oi": ("sbuf", [128, 24], F32),
-    "ov": ("sbuf", [128, 24], F32), "q4": ("sbuf", [128, 24], F32), "yoff": ("sbuf", [128, 24], U16),
-    "oc": ("sbuf", [128, 24], F32), "od": ("sbuf", [128, 24], F32), "offo": ("sbuf", [128, 96], U16),
-    "py0": ("sbuf", [128, 640], F32), "py1": ("sbuf", [128, 640], F32), "yo": ("sbuf", [128, 768], F32),
-    "pso": ("psum", [128, 1024], F32), "psr": ("psum", [128, 1024], F32),
-}
+F32, BF, U16, I32, CODES, PLANE = "float32", "bfloat16", "uint16", "int32", "float8_e4m3fn_x4", "uint8"
+SCRATCH = {}
+for _dt, _bufs in (
+    (F32, "tabp 32 jt 32 lutk 2560 ii 384 kk 384 nb 4 ab0 384 ab1 384 ab2 384 ab3 384 rr 4 yy 32 ft 32 pf 2 par0 1 r24 1 nq 1 a64 1 "
+          "i16 24 idx 24 ib 24 trash 24 iy 16 mask 16 cr0 8 b1 24 inr 24 tt 24 zero 24 ones 32 h0 12 h1 12 hs 12 ev 192 ind 24 "
+          "nind 24 cc 24 p1 24 rp 32 rt 32 ww 24 w0 12 w1 12 ws2 12 mm 16 base 1 sf 384 cw 528 dd 128 dtr 128 lq 4 ls 16 lin 16 "
+          "sg 768 sgt 768 q0 24 q1 24 qa 24 q2 24 qb 24 q3 24 oe 24 oa 24 om 24 oi 24 ov 24 q4 24 oc 24 od 24 py0 640 py1 640 yo 768"),
+    (I32, "tabi 24 pci 1 pbi 2"),
+    (U16, "offk 24 cr 8 hoff 12 zo 12 zu 24 offx 64 fd 48 yoff 24 offo 96"),
+    (BF, "xs 2048 ws 1024 hx 1024 ho 1536"),
+    (CODES, "qw 256 qx 256 qo 384 qr 256"),
+    (PLANE, "sw 256 sx 256 so 384 sr 256"),
+):
+    _w = _bufs.split()
+    for _i in range(0, len(_w), 2):
+        SCRATCH[_w[_i]] = ("sbuf", [128, int(_w[_i + 1])], _dt)
+SCRATCH["pso"] = ("psum", [128, 1024], F32)
+SCRATCH["psr"] = ("psum", [128, 1024], F32)
 SEMAPHORES = ["cv", "cs", "cg", "ct", "dw", "dx", "dwt", "dy", "lloc", "larr", "cloc", "carr"]
 
 
@@ -76,23 +59,29 @@ def rank_program(g, core, T, topo):
     g.sync.dma_start(T.xs[:, :], T.x[:, :]).then_inc(T.sem.dx, 16)
     g.sync.dma_start(T.ws[:, :], T.w[:, :]).then_inc(T.sem.dwt, 16)
 
-    L0 = op("g", [], G.iota, T.lutk[:, 0:256], [[1024, 256]], 0, 0, allow_small_or_imprecise_dtypes=True)
-    L1 = op("g", [], G.iota, T.lutk[:, 256:512], [[1024, 256]], 262144, 0, allow_small_or_imprecise_dtypes=True)
-    II = op("g", [], G.iota, T.ii[:, :], [[1, 384]], 0, 0, allow_small_or_imprecise_dtypes=True)
+    imp = dict(allow_small_or_imprecise_dtypes=True)
     PC = op("g", [], G.iota, T.pci[:, :], [[0, 1]], 0, 1)
-    I16 = op("g", [], G.iota, T.i16[:, :], [[16, 24]], 0, 0, allow_small_or_imprecise_dtypes=True)
-    IH0 = op("g", [], G.iota, T.ih0[:, :], [[32, 12]], CAPP, 0, allow_small_or_imprecise_dtypes=True)
-    CR0 = op("g", [], G.iota, T.cr0[:, :], [[16, 4], [0, 2]], 0, 0, allow_small_or_imprecise_dtypes=True)
+    L0 = op("g", [], G.iota, T.lutk[:, 0:256], [[1024, 256]], 0, 0, **imp)
+    II = op("g", [], G.iota, T.ii[:, :], [[1, 384]], 1, 0, **imp)
+    I16 = op("g", [], G.iota, T.i16[:, :], [[16, 24]], 1, 0, **imp)
+    IB = op("g", [], G.iota, T.ib[:, :], [[1, 24]], CAPP + 1, 0, **imp)
+    IY = op("g", [], G.iota, T.iy[:, :], [[1, 16]], 0, 0, **imp)
+    CR0 = op("g", [], G.iota, T.cr0[:, :], [[16, 4], [0, 2]], 0, 0, **imp)
     TP0 = op("v", [], V.memset, T.tabp[:, 24:32], 0.0)
-    NQ = [op("v", [], V.memset, T.nq[32 * a:32 * a + 32, :], float(-peers[a])) for a in range(P)]
-    lk = [L0, L1]
-    for k in range(2, 6):
-        lk.append(op("v", [L0], V.tensor_scalar, T.lutk[:, 256 * k:256 * k + 256], T.lutk[:, 0:256], 262144.0 * k, None, A.add))
-    for k in range(6, 10):
-        lk.append(op("s", [L0], S.activation, T.lutk[:, 256 * k:256 * k + 256], T.lutk[:, 0:256], AF.Identity, bias=262144.0 * k))
-    ZR = op("s", [L1], S.activation, T.zero[:, :], T.lutk[:, 0:384], AF.Copy, scale=0.0)
-    IW = [op("v", [], V.memset, T.iw[:, 0:512], 1.0), op("v", [], V.memset, T.iw[:, 512:528], 0.0)]
+    NQ = [op("v", [], V.memset, T.nq[32 * a:32 * a + 32, :], -peers[a] - 255.5 / 512) for a in range(P)]
+    PB = [op("v", [PC], V.tensor_scalar, T.pbi[:, 0:1], T.pci[:, :], 15, None, A.bitwise_and),
+          op("v", [], V.tensor_scalar, T.pbi[:, 1:2], T.pci[:, :], 4, 1, A.arith_shift_right, A.bitwise_and)]
+    Z24 = op("v", [], V.memset, T.zero[:, :], 0.0)
+    PF = op("v", [PB], V.tensor_copy, T.pf[:, :], T.pbi[:, :])
+    O32 = op("v", [], V.memset, T.ones[:, :], 1.0)
+    LO = op("v", [PF], V.tensor_scalar, T.par0[:, :], T.pf[:, 1:2], -1.0, 1.0, A.mult, A.add)
+    R24 = op("v", [PF], V.tensor_scalar, T.r24[:, :], T.pf[:, 0:1], 24.0, None, A.mult)
     CW0 = op("v", [], V.memset, T.cw[:, 0:CAPP], 0.0)
+    lk = [L0]
+    for k in range(1, 5):
+        lk.append(op("v", [L0], V.tensor_scalar, T.lutk[:, 256 * k:256 * k + 256], T.lutk[:, 0:256], 262144.0 * k, None, A.add))
+    for k in range(5, 10):
+        lk.append(op("s", [L0], S.activation, T.lutk[:, 256 * k:256 * k + 256], T.lutk[:, 0:256], AF.Identity, bias=262144.0 * k))
 
     OK = op("v", [DW], V.tensor_copy, T.offk[:, :], T.tabi[:, :])
     TP = op("v", [], V.tensor_copy, T.tabp[:, 0:24], T.tabi[:, :])
@@ -100,65 +89,53 @@ def rank_program(g, core, T, topo):
     KK = op("v", [OK, II, lk], V.tensor_tensor, T.kk[:, :], T.lutk[:, 0:2560].indirect(T.offk[:, 0:24]), T.ii[:, :], A.add)
     NB = [op("s", [JT], S.activation, T.nb[32 * a:32 * a + 32, :], T.jt[32 * a:32 * a + 32, 4 * a:4 * a + 4], AF.Copy, scale=-1024.0)
           for a in range(P)]
-    PB = [op("v", [PC], V.tensor_scalar, T.pbi[:, 0:1], T.pci[:, :], 15, None, A.bitwise_and),
-          op("v", [], V.tensor_scalar, T.pbi[:, 1:2], T.pci[:, :], 31, None, A.bitwise_and),
-          op("v", [], V.tensor_scalar, T.pbi[:, 2:3], T.pci[:, :], 4, 1, A.arith_shift_right, A.bitwise_and)]
-    E1 = op("v", [TP, NQ], V.tensor_scalar, T.e1[:, :], T.tabp[:, 0:24], 1.0 / 512, T.nq[:, 0:1], A.mult, A.add)
-    PF = op("v", [PB], V.tensor_copy, T.pf[:, :], T.pbi[:, :])
-    AB = [op("s", [NB, KK], S.activation, T.ab0[:, :], T.kk[:, :], AF.Abs, bias=T.nb[:, 0:1])]
-    A1 = op("s", [E1], S.activation, T.a1[:, :], T.e1[:, :], AF.Abs, bias=T.zero[:, 0:1]) if False else None
-    E1C = op("v", [E1], V.tensor_scalar, T.bb[:, :], T.e1[:, :], 255.5 / 512, None, A.subtract)
+    B1 = op("s", [NQ, TP], S.activation, T.b1[:, :], T.tabp[:, 0:24], AF.Abs, bias=T.nq[:, 0:1], scale=1.0 / 512)
+    EH0 = op("s", [LO], S.activation, T.h0[:, :], T.tabp[:, 0:12], AF.Copy, scale=T.par0[:, 0:1])
+    EH1 = op("s", [], S.activation, T.h1[:, :], T.tabp[:, 12:24], AF.Copy, scale=T.pf[:, 1:2])
+    AB = [op("s", [NB, KK], S.activation, T["ab%d" % k][:, :], T.kk[:, :], AF.Abs, bias=T.nb[:, k:k + 1]) for k in range(P)]
+    INR = op("v", [B1], V.tensor_scalar, T.inr[:, :], T.b1[:, :], 0.5, None, A.is_lt)
     IDX = op("v", [PF, I16], V.tensor_scalar, T.idx[:, :], T.i16[:, :], T.pf[:, 0:1], None, A.add)
-    A1 = op("s", [E1C], S.activation, T.a1[:, :], T.bb[:, :], AF.Abs)
-    for k in range(1, 4):
-        AB.append(op("s", [], S.activation, T["ab%d" % k][:, :], T.kk[:, :], AF.Abs, bias=T.nb[:, k:k + 1]))
-    RR = [op("v", [AB[0]], V.tensor_reduce, T.rr[:, 0:1], T.ab0[:, :], X, A.min)]
-    BB = op("v", [A1], V.tensor_scalar, T.nbb[:, :], T.a1[:, :], 0.5, None, A.is_lt)
-    BO = op("v", [A1], V.tensor_scalar, T.bb[:, :], T.a1[:, :], 0.5, None, A.is_gt)
-    RR.append(op("v", [AB[1]], V.tensor_reduce, T.rr[:, 1:2], T.ab1[:, :], X, A.min))
-    EL = op("v", [BO, E1], V.tensor_tensor, T.el[:, :], T.bb[:, :], T.e1[:, :], A.max)
-    for k in range(2, 4):
-        RR.append(op("v", [AB[k]], V.tensor_reduce, T.rr[:, k:k + 1], T["ab%d" % k][:, :], X, A.min))
-    YY = []
-    for d in range(P):
-        for a in range(P):
-            o_, i_ = T.yy[32 * d:32 * d + 32, 4 * a:4 * a + 4], T.rr[32 * a:32 * a + 32, 0:4]
-            if d % 2 == 0:
-                YY.append(op("v", [RR], V.tensor_copy, o_, i_))
-            else:
-                YY.append(op("s", [RR], S.activation, o_, i_, AF.Copy))
+    EHS = op("v", [EH0, EH1], V.tensor_tensor, T.hs[:, :], T.h0[:, :], T.h1[:, :], A.add)
+    TT = op("v", [IDX, INR], V.tensor_tensor, T.tt[:, :], T.idx[:, :], T.inr[:, :], A.mult)
+    EHO = op("v", [EHS], V.tensor_copy, T.hoff[:, :], T.hs[:, :])
+    TR = op("v", [IB, R24], V.tensor_scalar, T.trash[:, :], T.ib[:, :], T.r24[:, 0:1], None, A.add)
+    MK = op("v", [IY, PF], V.tensor_scalar, T.mask[:, :], T.iy[:, :], T.pf[:, 0:1], None, A.is_lt)
+    RR = [op("v", [AB[k]], V.tensor_reduce, T.rr[:, k:k + 1], T["ab%d" % k][:, :], X, A.min) for k in range(P)]
+    EV = op("s", [EHO, lk], S.activation, T.ev[:, :], T.lutk[:, 0:2560].indirect(T.hoff[:, 0:12]), AF.Copy)
+
+    def quarters(dst, src, deps):
+        out = []
+        for d in range(P):
+            for a in range(P):
+                o_, i_ = dst[32 * d:32 * d + 32, 4 * a:4 * a + 4], src[32 * a:32 * a + 32, 0:4]
+                if d % 2 == 0:
+                    out.append(op("v", deps, V.tensor_copy, o_, i_))
+                else:
+                    out.append(op("s", deps, S.activation, o_, i_, AF.Copy))
+        return out
+
+    YY = quarters(T.yy, T.rr, [RR])
     YD = op("v", [YY], V.tensor_copy, T.yy[:, 16:32], T.yy[:, 0:16])
     FT = op("v", [YD], V.transpose, T.ft[:, :], T.yy[:, :])
-    G1 = op("v", [FT, IDX], V.tensor_tensor, T.g1[:, :], T.idx[:, :], T.ft[:, 0:24], A.subtract)
-    S1 = op("v", [G1, EL], V.tensor_tensor, T.s1[:, :], T.g1[:, :], T.el[:, :], A.max)
-    OF = op("v", [S1], V.tensor_scalar, T.off[:, :], T.s1[:, :], 512.0, 512.0, A.mult, A.min)
-    IN = op("s", [OF, IW], S.activation, T.ind[:, :], T.iw[:, 0:528].indirect(T.off[:, 0:24]), AF.Copy)
-    P0 = op("v", [PF], V.tensor_scalar, T.par0[:, :], T.pf[:, 2:3], -1.0, 1.0, A.mult, A.add)
-    H1 = op("v", [S1], V.tensor_scalar, T.h1[:, :], T.s1[:, 1:24:2], T.pf[:, 2:3], None, A.mult)
-    H0 = op("v", [P0], V.tensor_scalar, T.h0[:, :], T.s1[:, 0:24:2], T.par0[:, 0:1], None, A.mult)
-    HS = op("v", [H0, H1], V.tensor_tensor, T.hs[:, :], T.h0[:, :], T.h1[:, :], A.add)
-    HO = op("v", [HS], V.tensor_scalar, T.hoff[:, :], T.hs[:, :], 512.0, 512.0, A.mult, A.min)
-    EV = op("s", [HO, lk], S.activation, T.ev[:, :], T.lutk[:, 0:528].indirect(T.hoff[:, 0:12]), AF.Copy)
-    HN = op("v", [HS], V.tensor_scalar, T.hn[:, :], T.hs[:, :], 1.0, None, A.is_ge)
-    IH = op("v", [IH0, PF], V.tensor_scalar, T.ih[:, :], T.ih0[:, :], T.pf[:, 1:2], None, A.add)
-    VT = op("v", [HN, IH], V.tensor_tensor, T.vt[:, :], T.hn[:, :], T.ih[:, :], A.mult)
+    IN = op("v", [FT, TT], V.tensor_tensor, T.ind[:, :], T.ft[:, 0:24], T.tt[:, :], A.is_equal)
+    NI = op("v", [FT, TT], V.tensor_tensor, T.nind[:, :], T.ft[:, 0:24], T.tt[:, :], A.not_equal)
+    CC = op("v", [IN, Z24], V.tensor_tensor_scan, T.cc[:, :], T.ind[:, :], T.zero[:, :], -1.0, A.add, A.add)
+    P1 = op("v", [NI, TR], V.tensor_tensor, T.p1[:, :], T.nind[:, :], T.trash[:, :], A.mult)
+    RP = op("v", [CC, O32], V.tensor_scalar, T.rp[:, :], T.ones[:, :], T.cc[:, 23:24], None, A.add)
+    WW = op("v", [P1, CC], V.tensor_tensor, T.ww[:, :], T.cc[:, :], T.p1[:, :], A.add)
+    RT = op("v", [RP], V.transpose, T.rt[:, :], T.rp[:, :])
+    W0 = op("s", [WW, LO], S.activation, T.w0[:, :], T.ww[:, 0:12], AF.Copy, scale=T.par0[:, 0:1])
+    W1 = op("v", [WW], V.tensor_scalar, T.w1[:, :], T.ww[:, 12:24], T.pf[:, 1:2], None, A.mult)
+    MM = op("v", [RT, MK], V.tensor_tensor, T.mm[:, :], T.rt[:, 0:16], T.mask[:, :], A.mult)
+    WS = op("v", [W0, W1], V.tensor_tensor, T.ws2[:, :], T.w0[:, :], T.w1[:, :], A.add)
+    BS = op("v", [MM], V.tensor_reduce, T.base[:, :], T.mm[:, :], X, A.add)
     CR = op("v", [CR0, PF], V.tensor_scalar, T.cr[:, :], T.cr0[:, :], T.pf[:, 0:1], None, A.add)
-    SS = op("v", [IN, ZR], V.tensor_tensor_scan, T.ss[:, :], T.ind[:, :], T.zero[:, :], -1.0, A.add, A.add)
-    ST = op("v", [SS], V.transpose, T.st[:, :], T.ss[:, :])
-    ZF = op("v", [ST, VT], V.tensor_tensor, T.zf[:, :], T.st[:, 0:384:32], T.vt[:, :], A.max)
-    ZO = op("v", [ZF], V.tensor_copy, T.zo[:, :], T.zf[:, :])
-    CW = op("v", [ZO, EV, CW0], V.tensor_copy, T.cw[:, 0:448].indirect(T.zo[:, 0:12]), T.ev[:, :])
+    ZO = op("v", [WS, BS], V.tensor_scalar, T.zo[:, :], T.ws2[:, :], T.base[:, 0:1], None, A.add)
+    CW = op("v", [ZO, EV, CW0], V.tensor_copy, T.cw[:, 0:528].indirect(T.zo[:, 0:12]), T.ev[:, :])
     DD = op("v", [CW, CR], V.tensor_copy, T.dd[:, :], T.cw[:, 0:CAPP].indirect(T.cr[:, 0:8]))
     DT = op("v", [DD], V.transpose, T.dtr[:, :], T.dd[:, :])
     LQ = op("v", [DT], V.tensor_tensor, T.lq[:, :], T.dtr[:, 0:128:32], T.dtr[:, 16:128:32], A.add)
-    LS = []
-    for d in range(P):
-        for a in range(P):
-            o_, i_ = T.ls[32 * d:32 * d + 32, 4 * a:4 * a + 4], T.lq[32 * a:32 * a + 32, 0:4]
-            if d % 2 == 0:
-                LS.append(op("v", [LQ], V.tensor_copy, o_, i_))
-            else:
-                LS.append(op("s", [LQ], S.activation, o_, i_, AF.Copy))
+    LS = quarters(T.ls, T.lq, [LQ])
     need("g", [LS])
 
     def send(items, local):
@@ -179,16 +156,18 @@ def rank_program(g, core, T, topo):
     send([(a, (T.ls[:, 4 * a:4 * a + 4], T.lin[:, 4 * back[a]:4 * back[a] + 4], T.sem.larr)) for a in range(P)], T.sem.lloc)
 
     QW = op("v", [DWT], V.quantize_mx, T.qw[:, :], T.sw[:, :], T.ws[:, :])
-    FD = [op("v", [FT], V.tensor_copy, T.fd[:, 0:48:2], T.ft[:, 0:24]), op("v", [], V.tensor_copy, T.fd[:, 1:48:2], T.ft[:, 0:24])]
-    SG = op("s", [FD, SS], S.activation, T.sg[:, :], T.ss[:, 0:384].indirect(T.fd[:, 0:48]), AF.Copy)
+    FD = [op("v", [FT], V.tensor_scalar, T.fd[:, h:48:2], T.ft[:, 0:24], -1.0, None, A.add) for h in range(2)]
+    ZU = op("v", [WW, BS], V.tensor_scalar, T.zu[:, :], T.ww[:, :], T.base[:, 0:1], None, A.add)
+    SF = op("s", [ZU, lk], S.activation, T.sf[:, :], T.lutk[:, 0:528].indirect(T.zu[:, 0:24]), AF.Copy)
     A64 = [op("v", [], V.memset, T.a64[32 * a:32 * a + 32, :], float(CAPP * a)) for a in range(P)]
     OC = op("v", [TP], V.tensor_scalar, T.oc[:, :], T.tabp[:, 0:24], 4.0, float(-4 * TB * r), A.mult, A.add)
     OD = op("v", [OC], V.tensor_scalar, T.od[:, :], T.oc[:, :], 0.0, float(4 * TB - 4), A.max, A.min)
     OO = [op("v", [OD], V.tensor_scalar, T.offo[:, 24 * t:24 * t + 24], T.od[:, :], float(t), None, A.add) for t in range(4)]
 
     LA = ("larr", P * ne)
-    OX = [op("v", [LA], V.tensor_scalar, T.offx[:, 16 * t:16 * t + 16], T.lin[:, :], 1.0 / 256, float(t), A.mult, A.add) for t in range(4)]
-    HX = []
+    OX, HX = {}, []
+    for t in (2, 3, 0, 1):
+        OX[t] = op("v", [LA], V.tensor_scalar, T.offx[:, 16 * t:16 * t + 16], T.lin[:, :], 1.0 / 256, float(t - 4 * TB * r), A.mult, A.add)
     for t in range(4):
         o_, i_ = T.hx[:, t:1024:4], T.xs[:, 0:2048].indirect(T.offx[:, 16 * t:16 * t + 16])
         if t < 2:
@@ -208,19 +187,20 @@ def rank_program(g, core, T, topo):
             HO_.append(op("v", [OO[t]], V.tensor_copy, o_, i_))
         else:
             HO_.append(op("s", [OO[t]], S.activation, o_, i_, AF.Copy))
+    SG = op("s", [FD, SF], S.activation, T.sg[:, :], T.sf[:, 0:384].indirect(T.fd[:, 0:48]), AF.Copy)
     QO = op("v", [HO_], V.quantize_mx, T.qo[:, :], T.so[:, :], T.ho[:, :])
     MO = [op("t", [QO, QW], M.matmul_mx, T.pso[:, 512 * o:512 * o + 384], T.qw[:, 128 * o:128 * o + 128], T.sw[:, 128 * o:128 * o + 128],
              T.qo[:, :], T.so[:, :], True, True) for o in range(O)]
     SGT = op("v", [SG], V.transpose, T.sgt[:, :], T.sg[:, :])
-    Q0 = op("v", [SGT, A64], V.tensor_scalar, T.q0[:, :], T.sgt[:, 0:768:32], T.a64[:, 0:1], None, A.add)
-    Q1 = op("v", [Q0, BB], V.tensor_tensor, T.q1[:, :], T.q0[:, :], T.nbb[:, :], A.mult)
+    Q0 = op("v", [SGT, A64], V.tensor_scalar, T.q0[:, :], T.sgt[:, 0:768:32], 1.0 / 1024, T.a64[:, 0:1], A.mult, A.add)
+    Q1 = op("v", [Q0, INR], V.tensor_tensor, T.q1[:, :], T.q0[:, :], T.inr[:, :], A.mult)
     QA = [op("v", [Q1], V.tensor_copy, T.qa[64 * h:64 * h + 64, :], T.q1[64 - 64 * h:128 - 64 * h, :]) for h in range(2)]
     OE = op("v", [TP], V.tensor_scalar, T.oe[:, :], T.tabp[:, 0:24], float(TB * r), None, A.is_ge)
     OA = op("v", [TP], V.tensor_scalar, T.oa[:, :], T.tabp[:, 0:24], float(TB * r + TB), None, A.is_lt)
     Q2 = op("v", [QA, Q1], V.tensor_tensor, T.q2[:, :], T.q1[:, :], T.qa[:, :], A.add)
     OM = op("v", [OE, OA], V.tensor_tensor, T.om[:, :], T.oe[:, :], T.oa[:, :], A.mult)
     QB = [op("v", [Q2], V.tensor_copy, T.qb[32 * a:32 * a + 32, :], T.q2[32 * (a ^ 1):32 * (a ^ 1) + 32, :]) for a in range(P)]
-    OI = op("v", [IDX], V.tensor_scalar, T.oi[:, :], T.idx[:, :], float(CAPP * P), None, A.add)
+    OI = op("v", [IDX], V.tensor_scalar, T.oi[:, :], T.idx[:, :], float(CAPP * P - 1), None, A.add)
     Q3 = op("v", [QB, Q2], V.tensor_tensor, T.q3[:, :], T.q2[:, :], T.qb[:, :], A.add)
     OV = op("v", [OM, OI], V.tensor_tensor, T.ov[:, :], T.om[:, :], T.oi[:, :], A.mult)
     Q4 = op("v", [Q3, OV], V.tensor_tensor, T.q4[:, :], T.q3[:, :], T.ov[:, :], A.add)

@@ -7,13 +7,14 @@ P = 4
 F32, BF, U16, I32, CODES, PLANE = "float32", "bfloat16", "uint16", "int32", "float8_e4m3fn_x4", "uint8"
 SCRATCH = {}
 for _dt, _bufs in (
-    (F32, "tabp 32 jt 32 lutk 2560 ii 384 kk 384 nb 4 ab0 384 ab1 384 ab2 384 ab3 384 rr 4 yy 32 ft 32 pf 2 par0 1 r24 1 nq 1 a64 1 "
-          "i16 24 idx 24 ib 24 trash 24 iy 16 mask 16 cr0 8 b1 24 inr 24 tt 24 zero 24 ones 32 h0 12 h1 12 hs 12 ev 192 ind 24 "
-          "nind 24 cc 24 p1 24 rp 32 rt 32 ww 24 w0 12 w1 12 ws2 12 mm 16 base 1 sf 384 cw 528 dd 128 dtr 128 lq 4 ls 16 lin 16 "
-          "sg 768 sgt 768 q0 24 q1 24 qa 24 q2 24 qb 24 q3 24 oe 24 oa 24 om 24 oi 24 ov 24 q4 24 oc 24 od 24 py0 640 py1 640 yo 768"),
-    (I32, "tabi 24 pci 1 pbi 2"),
-    (U16, "offk 24 cr 8 hoff 12 zo 12 zu 24 offx 64 fd 48 yoff 24 offo 96"),
-    (BF, "xs 2048 ws 1024 hx 1024 ho 1536"),
+    (F32, "tabp 24 mj 24 scr 24 gm 24 lutk 2560 ii 384 kk 384 nb 3 ab0 128 ab1 256 ab2 384 rr 3 yy 12 "
+          "pf 4 par0 1 t12 1 g1k 1 nq 1 a64 1 i16 24 idx 12 trash 12 mask 32 cr0 8 b1 12 sgn 12 inr 12 tt 12 zero 12 ones 32 "
+          "h0 12 h1 12 ey 12 ev 192 ind 12 nind 12 cc 12 p1 12 rp 32 rt 32 ww 12 mm 32 base 1 zf 32 zt 32 sf 512 cw 512 "
+          "dd 128 dtr 128 lq 4 ls 16 lin 16 fa16 12 fdf 12 sg 384 sgt 384 b1n 24 inrn 24 "
+          "q0 24 q1 24 qa 24 q2 24 qb 24 q3 24 oe 24 oa 24 om 24 oi 24 ov 24 q4 24 oc 24 od 24 py0 640 py1 640 yo 768"),
+    (I32, "tabi 24 pci 1 pbi 4 fi 12 fa 12 fb 12"),
+    (U16, "offk 24 cr 8 hoff 12 zo 12 zu 32 offx 32 fd 24 yoff 24 offo 48"),
+    (BF, "xs 2048 x2 2064 ws 1024 hx 1024 ho 1536"),
     (CODES, "qw 256 qx 256 qo 384 qr 256"),
     (PLANE, "sw 256 sx 256 so 384 sr 256"),
 ):
@@ -21,8 +22,8 @@ for _dt, _bufs in (
     for _i in range(0, len(_w), 2):
         SCRATCH[_w[_i]] = ("sbuf", [128, int(_w[_i + 1])], _dt)
 SCRATCH["pso"] = ("psum", [128, 1024], F32)
-SCRATCH["psr"] = ("psum", [128, 1024], F32)
-SEMAPHORES = ["cv", "cs", "cg", "ct", "dw", "dx", "dwt", "dy", "lloc", "larr", "cloc", "carr"]
+SCRATCH["psr"] = ("psum", [128, 2048], F32)
+SEMAPHORES = ["cv", "cs", "cg", "ct", "dw", "dx", "dwt", "dy", "lloc", "larr", "cloc", "carr0", "carr1"]
 
 
 def rank_program(g, core, T, topo):
@@ -55,28 +56,26 @@ def rank_program(g, core, T, topo):
 
     for i in range(8):
         (g.sync if i % 2 == 0 else g.scalar).dma_start(T.tabi[16 * i:16 * i + 16, 0:24], T.want[:, :]).then_inc(T.sem.dw, 16)
-    DW, DX, DWT = ("dw", 128), ("dx", 16), ("dwt", 16)
+    DW, DX, DWT = ("dw", 128), ("dx", 32), ("dwt", 16)
     g.sync.dma_start(T.xs[:, :], T.x[:, :]).then_inc(T.sem.dx, 16)
+    g.sync.dma_start(T.x2[:, 14:2062], T.x[:, :]).then_inc(T.sem.dx, 16)
     g.sync.dma_start(T.ws[:, :], T.w[:, :]).then_inc(T.sem.dwt, 16)
 
     imp = dict(allow_small_or_imprecise_dtypes=True)
     PC = op("g", [], G.iota, T.pci[:, :], [[0, 1]], 0, 1)
     L0 = op("g", [], G.iota, T.lutk[:, 0:256], [[1024, 256]], 0, 0, **imp)
     II = op("g", [], G.iota, T.ii[:, :], [[1, 384]], 1, 0, **imp)
-    I16 = op("g", [], G.iota, T.i16[:, :], [[16, 24]], 1, 0, **imp)
-    IB = op("g", [], G.iota, T.ib[:, :], [[1, 24]], CAPP + 1, 0, **imp)
-    IY = op("g", [], G.iota, T.iy[:, :], [[1, 16]], 0, 0, **imp)
     CR0 = op("g", [], G.iota, T.cr0[:, :], [[16, 4], [0, 2]], 0, 0, **imp)
-    TP0 = op("v", [], V.memset, T.tabp[:, 24:32], 0.0)
-    NQ = [op("v", [], V.memset, T.nq[32 * a:32 * a + 32, :], -peers[a] - 255.5 / 512) for a in range(P)]
+    I16 = op("g", [], G.iota, T.i16[:, :], [[16, 24]], 0, 0, **imp)
     PB = [op("v", [PC], V.tensor_scalar, T.pbi[:, 0:1], T.pci[:, :], 15, None, A.bitwise_and),
-          op("v", [], V.tensor_scalar, T.pbi[:, 1:2], T.pci[:, :], 4, 1, A.arith_shift_right, A.bitwise_and)]
-    Z24 = op("v", [], V.memset, T.zero[:, :], 0.0)
+          op("v", [], V.tensor_scalar, T.pbi[:, 1:2], T.pci[:, :], 4, 1, A.arith_shift_right, A.bitwise_and),
+          op("v", [], V.tensor_scalar, T.pbi[:, 2:3], T.pci[:, :], 4, None, A.arith_shift_right),
+          op("v", [], V.tensor_scalar, T.pbi[:, 3:4], T.pci[:, :], 31, None, A.bitwise_and)]
     PF = op("v", [PB], V.tensor_copy, T.pf[:, :], T.pbi[:, :])
-    O32 = op("v", [], V.memset, T.ones[:, :], 1.0)
     LO = op("v", [PF], V.tensor_scalar, T.par0[:, :], T.pf[:, 1:2], -1.0, 1.0, A.mult, A.add)
-    R24 = op("v", [PF], V.tensor_scalar, T.r24[:, :], T.pf[:, 0:1], 24.0, None, A.mult)
-    CW0 = op("v", [], V.memset, T.cw[:, 0:CAPP], 0.0)
+    T12 = op("v", [PF], V.tensor_scalar, T.t12[:, :], T.pf[:, 3:4], 12.0, float(CAPP), A.mult, A.add)
+    G1K = op("v", [PF], V.tensor_scalar, T.g1k[:, :], T.pf[:, 2:3], 1024.0, None, A.mult)
+    GM = [op("v", [L0, G1K], V.tensor_scalar, T.gm[:, 8 * k:8 * k + 8], T.lutk[:, 0:8], T.g1k[:, 0:1], None, A.is_equal) for k in range(3)]
     lk = [L0]
     for k in range(1, 5):
         lk.append(op("v", [L0], V.tensor_scalar, T.lutk[:, 256 * k:256 * k + 256], T.lutk[:, 0:256], 262144.0 * k, None, A.add))
@@ -84,135 +83,157 @@ def rank_program(g, core, T, topo):
         lk.append(op("s", [L0], S.activation, T.lutk[:, 256 * k:256 * k + 256], T.lutk[:, 0:256], AF.Identity, bias=262144.0 * k))
 
     OK = op("v", [DW], V.tensor_copy, T.offk[:, :], T.tabi[:, :])
-    TP = op("v", [], V.tensor_copy, T.tabp[:, 0:24], T.tabi[:, :])
-    JT = op("v", [TP, TP0], V.transpose, T.jt[:, :], T.tabp[:, :])
+    MJ = op("v", [GM], V.tensor_tensor, T.mj[:, :], T.tabi[:, :], T.gm[:, :], A.mult)
+    TP = op("v", [], V.tensor_copy, T.tabp[:, :], T.tabi[:, :])
     KK = op("v", [OK, II, lk], V.tensor_tensor, T.kk[:, :], T.lutk[:, 0:2560].indirect(T.offk[:, 0:24]), T.ii[:, :], A.add)
-    NB = [op("s", [JT], S.activation, T.nb[32 * a:32 * a + 32, :], T.jt[32 * a:32 * a + 32, 4 * a:4 * a + 4], AF.Copy, scale=-1024.0)
-          for a in range(P)]
-    B1 = op("s", [NQ, TP], S.activation, T.b1[:, :], T.tabp[:, 0:24], AF.Abs, bias=T.nq[:, 0:1], scale=1.0 / 512)
-    EH0 = op("s", [LO], S.activation, T.h0[:, :], T.tabp[:, 0:12], AF.Copy, scale=T.par0[:, 0:1])
-    EH1 = op("s", [], S.activation, T.h1[:, :], T.tabp[:, 12:24], AF.Copy, scale=T.pf[:, 1:2])
-    AB = [op("s", [NB, KK], S.activation, T["ab%d" % k][:, :], T.kk[:, :], AF.Abs, bias=T.nb[:, k:k + 1]) for k in range(P)]
-    INR = op("v", [B1], V.tensor_scalar, T.inr[:, :], T.b1[:, :], 0.5, None, A.is_lt)
-    IDX = op("v", [PF, I16], V.tensor_scalar, T.idx[:, :], T.i16[:, :], T.pf[:, 0:1], None, A.add)
-    EHS = op("v", [EH0, EH1], V.tensor_tensor, T.hs[:, :], T.h0[:, :], T.h1[:, :], A.add)
-    TT = op("v", [IDX, INR], V.tensor_tensor, T.tt[:, :], T.idx[:, :], T.inr[:, :], A.mult)
-    EHO = op("v", [EHS], V.tensor_copy, T.hoff[:, :], T.hs[:, :])
-    TR = op("v", [IB, R24], V.tensor_scalar, T.trash[:, :], T.ib[:, :], T.r24[:, 0:1], None, A.add)
-    MK = op("v", [IY, PF], V.tensor_scalar, T.mask[:, :], T.iy[:, :], T.pf[:, 0:1], None, A.is_lt)
-    RR = [op("v", [AB[k]], V.tensor_reduce, T.rr[:, k:k + 1], T["ab%d" % k][:, :], X, A.min) for k in range(P)]
-    EV = op("s", [EHO, lk], S.activation, T.ev[:, :], T.lutk[:, 0:2560].indirect(T.hoff[:, 0:12]), AF.Copy)
+    NB = [op("s", [MJ], S.activation, T.scr[:, 8 * k:8 * k + 8], T.mj[:, 8 * k:8 * k + 8], AF.Copy, scale=-1024.0,
+             accum_out=T.nb[:, k:k + 1]) for k in range(3)]
+    EH0 = op("s", [TP, LO], S.activation, T.h0[:, :], T.tabp[:, 0:24:2], AF.Copy, scale=T.par0[:, 0:1])
+    EH1 = op("s", [], S.activation, T.h1[:, :], T.tabp[:, 1:24:2], AF.Copy, scale=T.pf[:, 1:2])
+    IDX = op("s", [II, PF], S.activation, T.idx[:, :], T.ii[:, 0:384:32], AF.Identity, bias=T.pf[:, 3:4])
+    TR = op("s", [T12], S.activation, T.trash[:, :], T.ii[:, 0:12], AF.Identity, bias=T.t12[:, 0:1])
+    NQ = [op("s", [L0], S.activation, T.nq[32 * a:32 * a + 32, :], T.lutk[32 * a:32 * a + 32, 0:1], AF.Identity,
+             bias=-peers[a] - 255.5 / 512, scale=0.0) for a in range(P)]
+    AB2 = op("s", [NB, KK], S.activation, T.ab2[:, :], T.kk[:, 0:384], AF.Abs, bias=T.nb[:, 2:3])
+    AB1 = op("s", [], S.activation, T.ab1[:, :], T.kk[:, 0:256], AF.Abs, bias=T.nb[:, 1:2])
+    AB0 = op("v", [NB, KK], V.tensor_scalar, T.ab0[:, :], T.kk[:, 0:128], T.nb[:, 0:1], None, A.add)
+    EY = op("v", [EH0, EH1], V.tensor_tensor, T.ey[:, :], T.h0[:, :], T.h1[:, :], A.add)
+    MK = op("v", [II, PF], V.tensor_scalar, T.mask[:, :], T.ii[:, 0:32], T.pf[:, 3:4], 0.5, A.subtract, A.is_lt)
+    RR = [op("v", [AB0], V.tensor_reduce, T.rr[:, 0:1], T.ab0[:, :], X, A.min, apply_absolute_value=True)]
+    EHO = op("v", [EY], V.tensor_copy, T.hoff[:, :], T.ey[:, :])
+    RR += [op("v", [AB2], V.tensor_reduce, T.rr[:, 2:3], T.ab2[:, :], X, A.min),
+           op("v", [AB1], V.tensor_reduce, T.rr[:, 1:2], T.ab1[:, :], X, A.min)]
+    B1 = op("s", [EY, NQ], S.activation, T.b1[:, :], T.ey[:, :], AF.Abs, bias=T.nq[:, 0:1], scale=1.0 / 512)
+    SGN = op("s", [B1], S.activation, T.sgn[:, :], T.b1[:, :], AF.Sign, bias=0.5, scale=-1.0)
+    INR = op("s", [SGN], S.activation, T.inr[:, :], T.sgn[:, :], AF.Relu)
 
-    def quarters(dst, src, deps):
+    def quarters(place, src, n, deps, give=()):
         out = []
         for d in range(P):
             for a in range(P):
-                o_, i_ = dst[32 * d:32 * d + 32, 4 * a:4 * a + 4], src[32 * a:32 * a + 32, 0:4]
-                if d % 2 == 0:
+                o_, i_ = place(d, a), src[32 * a:32 * a + 32, 0:n]
+                if d % 2 == 0 and (d, a) not in give:
                     out.append(op("v", deps, V.tensor_copy, o_, i_))
                 else:
                     out.append(op("s", deps, S.activation, o_, i_, AF.Copy))
         return out
 
-    YY = quarters(T.yy, T.rr, [RR])
-    YD = op("v", [YY], V.tensor_copy, T.yy[:, 16:32], T.yy[:, 0:16])
-    FT = op("v", [YD], V.transpose, T.ft[:, :], T.yy[:, :])
-    IN = op("v", [FT, TT], V.tensor_tensor, T.ind[:, :], T.ft[:, 0:24], T.tt[:, :], A.is_equal)
-    NI = op("v", [FT, TT], V.tensor_tensor, T.nind[:, :], T.ft[:, 0:24], T.tt[:, :], A.not_equal)
-    CC = op("v", [IN, Z24], V.tensor_tensor_scan, T.cc[:, :], T.ind[:, :], T.zero[:, :], -1.0, A.add, A.add)
+    YY = quarters(lambda d, a: T.yy[32 * d:32 * d + 32, a:12:4], T.rr, 3, [RR])
+    ZZ = op("s", [], S.activation, T.zero[:, :], T.ii[:, 0:12], AF.Copy, scale=0.0)
+    O32 = op("s", [], S.activation, T.ones[:, :], T.ii[:, 0:32], AF.Identity, bias=1.0, scale=0.0)
+    EV = op("s", [EHO, lk], S.activation, T.ev[:, :], T.lutk[:, 0:2560].indirect(T.hoff[:, 0:12]), AF.Copy)
+    CW0 = op("s", [], S.activation, T.cw[:, 0:CAPP], T.ii[:, 0:CAPP], AF.Copy, scale=0.0)
+    TT = op("v", [IDX, INR], V.tensor_tensor, T.tt[:, :], T.idx[:, :], T.inr[:, :], A.mult)
+    IN = op("v", [YY, TT], V.tensor_tensor, T.ind[:, :], T.yy[:, :], T.tt[:, :], A.is_equal)
+    NI = op("v", [], V.tensor_tensor, T.nind[:, :], T.yy[:, :], T.tt[:, :], A.not_equal)
+    CC = op("v", [IN, ZZ], V.tensor_tensor_scan, T.cc[:, :], T.ind[:, :], T.zero[:, :], -1.0, A.add, A.add)
     P1 = op("v", [NI, TR], V.tensor_tensor, T.p1[:, :], T.nind[:, :], T.trash[:, :], A.mult)
-    RP = op("v", [CC, O32], V.tensor_scalar, T.rp[:, :], T.ones[:, :], T.cc[:, 23:24], None, A.add)
+    RP = op("v", [CC, O32], V.tensor_scalar, T.rp[:, :], T.ones[:, :], T.cc[:, 11:12], None, A.add)
     WW = op("v", [P1, CC], V.tensor_tensor, T.ww[:, :], T.cc[:, :], T.p1[:, :], A.add)
     RT = op("v", [RP], V.transpose, T.rt[:, :], T.rp[:, :])
-    W0 = op("s", [WW, LO], S.activation, T.w0[:, :], T.ww[:, 0:12], AF.Copy, scale=T.par0[:, 0:1])
-    W1 = op("v", [WW], V.tensor_scalar, T.w1[:, :], T.ww[:, 12:24], T.pf[:, 1:2], None, A.mult)
-    MM = op("v", [RT, MK], V.tensor_tensor, T.mm[:, :], T.rt[:, 0:16], T.mask[:, :], A.mult)
-    WS = op("v", [W0, W1], V.tensor_tensor, T.ws2[:, :], T.w0[:, :], T.w1[:, :], A.add)
+    MM = op("v", [RT, MK], V.tensor_tensor, T.mm[:, :], T.rt[:, :], T.mask[:, :], A.mult)
     BS = op("v", [MM], V.tensor_reduce, T.base[:, :], T.mm[:, :], X, A.add)
+    ZO = op("v", [WW, BS], V.tensor_scalar, T.zo[:, :], T.ww[:, :], T.base[:, 0:1], None, A.add)
     CR = op("v", [CR0, PF], V.tensor_scalar, T.cr[:, :], T.cr0[:, :], T.pf[:, 0:1], None, A.add)
-    ZO = op("v", [WS, BS], V.tensor_scalar, T.zo[:, :], T.ws2[:, :], T.base[:, 0:1], None, A.add)
-    CW = op("v", [ZO, EV, CW0], V.tensor_copy, T.cw[:, 0:528].indirect(T.zo[:, 0:12]), T.ev[:, :])
+    CW = op("v", [ZO, EV, CW0], V.tensor_copy, T.cw[:, 0:512].indirect(T.zo[:, 0:12]), T.ev[:, :])
     DD = op("v", [CW, CR], V.tensor_copy, T.dd[:, :], T.cw[:, 0:CAPP].indirect(T.cr[:, 0:8]))
     DT = op("v", [DD], V.transpose, T.dtr[:, :], T.dd[:, :])
     LQ = op("v", [DT], V.tensor_tensor, T.lq[:, :], T.dtr[:, 0:128:32], T.dtr[:, 16:128:32], A.add)
-    LS = quarters(T.ls, T.lq, [LQ])
+    LS = quarters(lambda d, a: T.ls[32 * d:32 * d + 32, 4 * a:4 * a + 4], T.lq, 4, [LQ])
     need("g", [LS])
 
     def send(items, local):
         tr = []
-        for a, (src, dst, sem) in items:
+        for j, (a, src, dst, sem) in enumerate(items):
             c = T.cores[peers[a]]
             rid, pid, _ = topo.addr(c)
             es = topo.engines(core, c)
-            n = len(es) // P
+            n = len(es) // len(items)
             m = 0
-            for e in es[a * n:a * n + n]:
+            for e in es[j * n:j * n + n]:
                 m |= 1 << e
             tr.append(RemoteDMATransfer(dst_ids=[DstId(rid=rid, pnc=pid)], dma_engine_mask=m, remote_sem=sem, src=src, dst=dst))
         g.remote_dma_fused(tr, local_sem=local)
 
     back = [(r - peers[a] - 1) % N for a in range(P)]
-    ne = len(topo.engines(core, T.cores[peers[0]])) // P
-    send([(a, (T.ls[:, 4 * a:4 * a + 4], T.lin[:, 4 * back[a]:4 * back[a] + 4], T.sem.larr)) for a in range(P)], T.sem.lloc)
+    ne = len(topo.engines(core, T.cores[peers[0]]))
+    send([(a, T.ls[:, 4 * a:4 * a + 4], T.lin[:, 4 * back[a]:4 * back[a] + 4], T.sem.larr) for a in range(P)], T.sem.lloc)
 
     QW = op("v", [DWT], V.quantize_mx, T.qw[:, :], T.sw[:, :], T.ws[:, :])
-    FD = [op("v", [FT], V.tensor_scalar, T.fd[:, h:48:2], T.ft[:, 0:24], -1.0, None, A.add) for h in range(2)]
-    ZU = op("v", [WW, BS], V.tensor_scalar, T.zu[:, :], T.ww[:, :], T.base[:, 0:1], None, A.add)
-    SF = op("s", [ZU, lk], S.activation, T.sf[:, :], T.lutk[:, 0:528].indirect(T.zu[:, 0:24]), AF.Copy)
-    A64 = [op("v", [], V.memset, T.a64[32 * a:32 * a + 32, :], float(CAPP * a)) for a in range(P)]
-    OC = op("v", [TP], V.tensor_scalar, T.oc[:, :], T.tabp[:, 0:24], 4.0, float(-4 * TB * r), A.mult, A.add)
+    ZF0 = op("v", [], V.memset, T.zf[:, :], 0.0)
+    FI = op("v", [YY], V.tensor_scalar, T.fi[:, :], T.yy[:, :], -1.0, None, A.add)
+    ZF = [op("v", [ZF0, WW, BS], V.tensor_scalar, T.zf[:, c:c + 12], T.ww[:, :], T.base[:, 0:1], None, A.add) for c in (0, 16)]
+    FA = op("v", [FI], V.tensor_scalar, T.fa[:, :], T.fi[:, :], 31, None, A.bitwise_and)
+    ZT = op("v", [ZF], V.transpose, T.zt[:, :], T.zf[:, :])
+    FB = op("v", [FI], V.tensor_scalar, T.fb[:, :], T.fi[:, :], 5, None, A.arith_shift_right)
+    ZU = op("v", [ZT], V.tensor_copy, T.zu[:, :], T.zt[:, :])
+    SF = op("s", [ZU, lk], S.activation, T.sf[:, :], T.lutk[:, 0:512].indirect(T.zu[:, 0:32]), AF.Copy)
+    OC = op("v", [TP], V.tensor_scalar, T.oc[:, :], T.tabp[:, :], 4.0, float(-4 * TB * r), A.mult, A.add)
+    FA6 = op("v", [FA], V.tensor_scalar, T.fa16[:, :], T.fa[:, :], 16.0, None, A.mult)
     OD = op("v", [OC], V.tensor_scalar, T.od[:, :], T.oc[:, :], 0.0, float(4 * TB - 4), A.max, A.min)
-    OO = [op("v", [OD], V.tensor_scalar, T.offo[:, 24 * t:24 * t + 24], T.od[:, :], float(t), None, A.add) for t in range(4)]
+    FDF = op("v", [FA6, FB], V.tensor_tensor, T.fdf[:, :], T.fa16[:, :], T.fb[:, :], A.add)
+    OO = [op("v", [OD], V.tensor_scalar, T.offo[:, 24 * t:24 * t + 24], T.od[:, :], float(t), None, A.add) for t in range(2)]
+    FD = [op("v", [FDF], V.tensor_copy, T.fd[:, h:24:2], T.fdf[:, :]) for h in range(2)]
 
-    LA = ("larr", P * ne)
-    OX, HX = {}, []
-    for t in (2, 3, 0, 1):
-        OX[t] = op("v", [LA], V.tensor_scalar, T.offx[:, 16 * t:16 * t + 16], T.lin[:, :], 1.0 / 256, float(t - 4 * TB * r), A.mult, A.add)
-    for t in range(4):
-        o_, i_ = T.hx[:, t:1024:4], T.xs[:, 0:2048].indirect(T.offx[:, 16 * t:16 * t + 16])
+    def gather(t, out, offsets, deps):
+        win = T.xs[:, 0:2046] if t < 2 else T.x2[:, 16:2062]
         if t < 2:
-            HX.append(op("v", [OX[t], DX], V.tensor_copy, o_, i_))
-        else:
-            HX.append(op("s", [OX[t], DX], S.activation, o_, i_, AF.Copy))
-    QX = op("v", [HX], V.quantize_mx, T.qx[:, :], T.sx[:, :], T.hx[:, :])
-    need("g", [QX])
-    send([(a, (T.qx[:, 64 * a:64 * a + 64].bitcast(dt.uint8), T.qr[:, 64 * back[a]:64 * back[a] + 64].bitcast(dt.uint8), T.sem.carr))
-          for a in range(P)], T.sem.cloc)
-    send([(a, (T.sx[:, 64 * a:64 * a + 64], T.sr[:, 64 * back[a]:64 * back[a] + 64], T.sem.carr)) for a in range(P)], T.sem.cloc)
+            return op("v", [deps[t % 2], DX], V.tensor_copy, out, win.indirect(offsets))
+        return op("s", [deps[t % 2], DX], S.activation, out, win.indirect(offsets), AF.Copy)
 
-    HO_ = []
-    for t in range(4):
-        o_, i_ = T.ho[:, t:1536:4], T.xs[:, 0:2048].indirect(T.offo[:, 24 * t:24 * t + 24])
-        if t < 2:
-            HO_.append(op("v", [OO[t]], V.tensor_copy, o_, i_))
-        else:
-            HO_.append(op("s", [OO[t]], S.activation, o_, i_, AF.Copy))
-    SG = op("s", [FD, SF], S.activation, T.sg[:, :], T.sf[:, 0:384].indirect(T.fd[:, 0:48]), AF.Copy)
+    LA = ("larr", ne)
+    OX = [op("v", [LA], V.tensor_scalar, T.offx[:, 16 * t:16 * t + 16], T.lin[:, :], 1.0 / 256, float(t - 4 * TB * r), A.mult, A.add)
+          for t in range(2)]
+    QX = []
+    for h in range(2):
+        HX = [gather(t, T.hx[:, 512 * h + t:512 * h + 512:4], T.offx[:, 16 * (t % 2) + 8 * h:16 * (t % 2) + 8 * h + 8], OX) for t in range(4)]
+        c = slice(128 * h, 128 * h + 128)
+        QX.append(op("v", [HX], V.quantize_mx, T.qx[:, c], T.sx[:, c], T.hx[:, 512 * h:512 * h + 512]))
+        need("g", [QX])
+        pair, sem = (2 * h, 2 * h + 1), T.sem["carr%d" % h]
+        send([(a, T.qx[:, 64 * a:64 * a + 64].bitcast(dt.uint8), T.qr[:, 64 * back[a]:64 * back[a] + 64].bitcast(dt.uint8), sem)
+              for a in pair], T.sem.cloc)
+        send([(a, T.sx[:, 64 * a:64 * a + 64], T.sr[:, 64 * back[a]:64 * back[a] + 64], sem) for a in pair], T.sem.cloc)
+
+    HO_ = [gather(t, T.ho[:, t:1536:4], T.offo[:, 24 * (t % 2):24 * (t % 2) + 24], OO) for t in range(4)]
+    SG = op("s", [FD, SF], S.activation, T.sg[:, :], T.sf[:, 0:512].indirect(T.fd[:, 0:24]), AF.Copy)
+    B1N = op("s", [NQ, TP], S.activation, T.b1n[:, :], T.tabp[:, :], AF.Abs, bias=T.nq[:, 0:1], scale=1.0 / 512)
     QO = op("v", [HO_], V.quantize_mx, T.qo[:, :], T.so[:, :], T.ho[:, :])
-    MO = [op("t", [QO, QW], M.matmul_mx, T.pso[:, 512 * o:512 * o + 384], T.qw[:, 128 * o:128 * o + 128], T.sw[:, 128 * o:128 * o + 128],
-             T.qo[:, :], T.so[:, :], True, True) for o in range(O)]
+
+    def product(o, out, codes, plane, deps):
+        return op("t", deps, M.matmul_mx, out, T.qw[:, 128 * o:128 * o + 128], T.sw[:, 128 * o:128 * o + 128], codes, plane, True, True)
+
+    MO = [product(o, T.pso[:, 512 * o:512 * o + 384], T.qo[:, :], T.so[:, :], [QO, QW]) for o in range(O)]
+    A64 = [op("v", [], V.memset, T.a64[32 * a:32 * a + 32, :], float(CAPP * a)) for a in range(P)]
+    OI = op("v", [I16], V.tensor_scalar, T.oi[:, :], T.i16[:, :], T.pf[:, 0:1], float(CAPP * P), A.add, A.add)
+    OE = op("v", [TP], V.tensor_scalar, T.oe[:, :], T.tabp[:, :], float(TB * r), None, A.is_ge)
+    OA = op("v", [TP], V.tensor_scalar, T.oa[:, :], T.tabp[:, :], float(TB * r + TB), None, A.is_lt)
     SGT = op("v", [SG], V.transpose, T.sgt[:, :], T.sg[:, :])
-    Q0 = op("v", [SGT, A64], V.tensor_scalar, T.q0[:, :], T.sgt[:, 0:768:32], 1.0 / 1024, T.a64[:, 0:1], A.mult, A.add)
-    Q1 = op("v", [Q0, INR], V.tensor_tensor, T.q1[:, :], T.q0[:, :], T.inr[:, :], A.mult)
-    QA = [op("v", [Q1], V.tensor_copy, T.qa[64 * h:64 * h + 64, :], T.q1[64 - 64 * h:128 - 64 * h, :]) for h in range(2)]
-    OE = op("v", [TP], V.tensor_scalar, T.oe[:, :], T.tabp[:, 0:24], float(TB * r), None, A.is_ge)
-    OA = op("v", [TP], V.tensor_scalar, T.oa[:, :], T.tabp[:, 0:24], float(TB * r + TB), None, A.is_lt)
-    Q2 = op("v", [QA, Q1], V.tensor_tensor, T.q2[:, :], T.q1[:, :], T.qa[:, :], A.add)
+    INN = op("v", [B1N], V.tensor_scalar, T.inrn[:, :], T.b1n[:, :], 0.5, None, A.is_lt)
+    Q0 = [op("v", [SGT, A64], V.tensor_scalar, T.q0[:, h:24:2], T.sgt[:, 16 * h:384:32], 1.0 / 1024, T.a64[:, 0:1], A.mult, A.add)
+          for h in range(2)]
     OM = op("v", [OE, OA], V.tensor_tensor, T.om[:, :], T.oe[:, :], T.oa[:, :], A.mult)
+    Q1 = op("v", [Q0, INN], V.tensor_tensor, T.q1[:, :], T.q0[:, :], T.inrn[:, :], A.mult)
+    QA = [op("v", [Q1], V.tensor_copy, T.qa[64 * h:64 * h + 64, :], T.q1[64 - 64 * h:128 - 64 * h, :]) for h in range(2)]
+    Q2 = op("v", [QA, Q1], V.tensor_tensor, T.q2[:, :], T.q1[:, :], T.qa[:, :], A.add)
     QB = [op("v", [Q2], V.tensor_copy, T.qb[32 * a:32 * a + 32, :], T.q2[32 * (a ^ 1):32 * (a ^ 1) + 32, :]) for a in range(P)]
-    OI = op("v", [IDX], V.tensor_scalar, T.oi[:, :], T.idx[:, :], float(CAPP * P - 1), None, A.add)
-    Q3 = op("v", [QB, Q2], V.tensor_tensor, T.q3[:, :], T.q2[:, :], T.qb[:, :], A.add)
     OV = op("v", [OM, OI], V.tensor_tensor, T.ov[:, :], T.om[:, :], T.oi[:, :], A.mult)
+    Q3 = op("v", [QB, Q2], V.tensor_tensor, T.q3[:, :], T.q2[:, :], T.qb[:, :], A.add)
     Q4 = op("v", [Q3, OV], V.tensor_tensor, T.q4[:, :], T.q3[:, :], T.ov[:, :], A.add)
     YO = op("v", [Q4], V.tensor_copy, T.yoff[:, :], T.q4[:, :])
     PO = [op("v", [MO[0]], V.tensor_copy, T.py0[:, 256:640], T.pso[:, 0:384]),
           op("s", [MO[1]], S.activation, T.py1[:, 256:640], T.pso[:, 512:896], AF.Copy)]
 
-    CA = ("carr", 2 * P * ne)
-    MR = [op("t", [CA, QW], M.matmul_mx, T.psr[:, 512 * o:512 * o + 256], T.qw[:, 128 * o:128 * o + 128], T.sw[:, 128 * o:128 * o + 128],
-             T.qr[:, :], T.sr[:, :], True, True) for o in range(O)]
-    PR = [op("v", [MR[0]], V.tensor_copy, T.py0[:, 0:256], T.psr[:, 0:256]),
-          op("s", [MR[1]], S.activation, T.py1[:, 0:256], T.psr[:, 512:768], AF.Copy)]
+    PR = [[], []]
+    for h in range(2):
+        c = 64 * min(back[2 * h], back[2 * h + 1])
+        for o in range(O):
+            b = 512 * (2 * h + o)
+            m = product(o, T.psr[:, b:b + 128], T.qr[:, c:c + 128], T.sr[:, c:c + 128], [("carr%d" % h, 2 * ne), QW])
+            if o == 0:
+                PR[0].append(op("v", [m], V.tensor_copy, T.py0[:, c:c + 128], T.psr[:, b:b + 128]))
+            else:
+                PR[1].append(op("s", [m], S.activation, T.py1[:, c:c + 128], T.psr[:, b:b + 128], AF.Copy))
     nd = 0
     for h in range(2):
         c = 192 * h
@@ -223,4 +244,4 @@ def rank_program(g, core, T, topo):
             g.sync.dma_start(T.y[:, 384 * o + c:384 * o + c + 192], T.yo[:, 384 * o + c:384 * o + c + 192]).then_inc(T.sem.dy, 16)
             nd += 16
     need("y", [("dy", nd)])
-    need("g", [("lloc", P * ne), ("cloc", 2 * P * ne)] + [("c" + q, cnt[q]) for q in cnt])
+    need("g", [("lloc", ne), ("cloc", 4 * ne)] + [("c" + q, cnt[q]) for q in cnt])

import numpy as np
from concourse.bass import DstId, RemoteDMATransfer
from concourse.mybir import dt, AluOpType, AxisListType, ActivationFunctionType

N, TB, NT, CAPP, O = 5, 512, 384, 64, 2
P = 4
F32, BF, U16, I32, CODES, PLANE = "float32", "bfloat16", "uint16", "int32", "float8_e4m3fn_x4", "uint8"
SCRATCH = {}
for _dt, _bufs in (
    (F32, "tabp 24 mj 24 scr 24 gm 24 lutk 2560 ii 384 kk 384 nb 3 ab0 128 ab1 256 ab2 384 rr 3 yy 12 "
          "pf 4 par0 1 t12 1 g1k 1 nq 1 a64 1 i16 24 idx 12 trash 12 mask 32 cr0 8 b1 12 sgn 12 inr 12 tt 12 zero 12 ones 32 "
          "h0 12 h1 12 ey 12 ev 192 ind 12 nind 12 cc 12 p1 12 rp 32 rt 32 ww 12 mm 32 base 1 zf 32 zt 32 sf 512 cw 512 "
          "dd 128 dtr 128 lq 4 ls 16 lin 16 fa16 12 fdf 12 sg 384 sgt 384 b1n 24 inrn 24 "
          "q0 24 q1 24 qa 24 q2 24 qb 24 q3 24 oe 24 oa 24 om 24 oi 24 ov 24 q4 24 oc 24 od 24 py0 640 py1 640 yo 768"),
    (I32, "tabi 24 pci 1 pbi 4 fi 12 fa 12 fb 12"),
    (U16, "offk 24 cr 8 hoff 12 zo 12 zu 32 offx 32 fd 24 yoff 24 offo 48"),
    (BF, "xs 2048 x2 2064 ws 1024 hx 1024 ho 1536"),
    (CODES, "qw 256 qx 256 qo 384 qr 256"),
    (PLANE, "sw 256 sx 256 so 384 sr 256"),
):
    _w = _bufs.split()
    for _i in range(0, len(_w), 2):
        SCRATCH[_w[_i]] = ("sbuf", [128, int(_w[_i + 1])], _dt)
SCRATCH["pso"] = ("psum", [128, 1024], F32)
SCRATCH["psr"] = ("psum", [128, 2048], F32)
SEMAPHORES = ["cv", "cs", "cg", "ct", "dw", "dx", "dwt", "dy", "lloc", "larr", "cloc", "carr0", "carr1"]


def rank_program(g, core, T, topo):
    r = T.rank_of(core)
    if r is None:
        return
    A, AF, X = AluOpType, ActivationFunctionType, AxisListType.X
    peers = [(r + 1 + a) % N for a in range(P)]
    eng = {"v": g.vector, "s": g.scalar, "g": g, "t": g.tensor, "y": g.sync}
    cnt = {"v": 0, "s": 0, "g": 0, "t": 0}
    seen = {q: {} for q in eng}

    def need(q, deps):
        for d in deps:
            if isinstance(d, list):
                need(q, d)
                continue
            sem, val = d
            if seen[q].get(sem, 0) < val:
                eng[q].wait_ge(T.sem[sem], val)
                seen[q][sem] = val

    def op(q, deps, fn, *args, **kw):
        need(q, deps)
        cnt[q] += 1
        fn(*args, **kw).then_inc(T.sem["c" + q], 1)
        return ("c" + q, cnt[q])

    V, S, G, M = g.vector, g.scalar, g, g.tensor

    for i in range(8):
        (g.sync if i % 2 == 0 else g.scalar).dma_start(T.tabi[16 * i:16 * i + 16, 0:24], T.want[:, :]).then_inc(T.sem.dw, 16)
    DW, DX, DWT = ("dw", 128), ("dx", 32), ("dwt", 16)
    g.sync.dma_start(T.xs[:, :], T.x[:, :]).then_inc(T.sem.dx, 16)
    g.sync.dma_start(T.x2[:, 14:2062], T.x[:, :]).then_inc(T.sem.dx, 16)
    g.sync.dma_start(T.ws[:, :], T.w[:, :]).then_inc(T.sem.dwt, 16)

    imp = dict(allow_small_or_imprecise_dtypes=True)
    PC = op("g", [], G.iota, T.pci[:, :], [[0, 1]], 0, 1)
    L0 = op("g", [], G.iota, T.lutk[:, 0:256], [[1024, 256]], 0, 0, **imp)
    II = op("g", [], G.iota, T.ii[:, :], [[1, 384]], 1, 0, **imp)
    CR0 = op("g", [], G.iota, T.cr0[:, :], [[16, 4], [0, 2]], 0, 0, **imp)
    I16 = op("g", [], G.iota, T.i16[:, :], [[16, 24]], 0, 0, **imp)
    PB = [op("v", [PC], V.tensor_scalar, T.pbi[:, 0:1], T.pci[:, :], 15, None, A.bitwise_and),
          op("v", [], V.tensor_scalar, T.pbi[:, 1:2], T.pci[:, :], 4, 1, A.arith_shift_right, A.bitwise_and),
          op("v", [], V.tensor_scalar, T.pbi[:, 2:3], T.pci[:, :], 4, None, A.arith_shift_right),
          op("v", [], V.tensor_scalar, T.pbi[:, 3:4], T.pci[:, :], 31, None, A.bitwise_and)]
    PF = op("v", [PB], V.tensor_copy, T.pf[:, :], T.pbi[:, :])
    LO = op("v", [PF], V.tensor_scalar, T.par0[:, :], T.pf[:, 1:2], -1.0, 1.0, A.mult, A.add)
    T12 = op("v", [PF], V.tensor_scalar, T.t12[:, :], T.pf[:, 3:4], 12.0, float(CAPP), A.mult, A.add)
    G1K = op("v", [PF], V.tensor_scalar, T.g1k[:, :], T.pf[:, 2:3], 1024.0, None, A.mult)
    GM = [op("v", [L0, G1K], V.tensor_scalar, T.gm[:, 8 * k:8 * k + 8], T.lutk[:, 0:8], T.g1k[:, 0:1], None, A.is_equal) for k in range(3)]
    lk = [L0]
    for k in range(1, 5):
        lk.append(op("v", [L0], V.tensor_scalar, T.lutk[:, 256 * k:256 * k + 256], T.lutk[:, 0:256], 262144.0 * k, None, A.add))
    for k in range(5, 10):
        lk.append(op("s", [L0], S.activation, T.lutk[:, 256 * k:256 * k + 256], T.lutk[:, 0:256], AF.Identity, bias=262144.0 * k))

    OK = op("v", [DW], V.tensor_copy, T.offk[:, :], T.tabi[:, :])
    MJ = op("v", [GM], V.tensor_tensor, T.mj[:, :], T.tabi[:, :], T.gm[:, :], A.mult)
    TP = op("v", [], V.tensor_copy, T.tabp[:, :], T.tabi[:, :])
    KK = op("v", [OK, II, lk], V.tensor_tensor, T.kk[:, :], T.lutk[:, 0:2560].indirect(T.offk[:, 0:24]), T.ii[:, :], A.add)
    NB = [op("s", [MJ], S.activation, T.scr[:, 8 * k:8 * k + 8], T.mj[:, 8 * k:8 * k + 8], AF.Copy, scale=-1024.0,
             accum_out=T.nb[:, k:k + 1]) for k in range(3)]
    EH0 = op("s", [TP, LO], S.activation, T.h0[:, :], T.tabp[:, 0:24:2], AF.Copy, scale=T.par0[:, 0:1])
    EH1 = op("s", [], S.activation, T.h1[:, :], T.tabp[:, 1:24:2], AF.Copy, scale=T.pf[:, 1:2])
    IDX = op("s", [II, PF], S.activation, T.idx[:, :], T.ii[:, 0:384:32], AF.Identity, bias=T.pf[:, 3:4])
    TR = op("s", [T12], S.activation, T.trash[:, :], T.ii[:, 0:12], AF.Identity, bias=T.t12[:, 0:1])
    NQ = [op("s", [L0], S.activation, T.nq[32 * a:32 * a + 32, :], T.lutk[32 * a:32 * a + 32, 0:1], AF.Identity,
             bias=-peers[a] - 255.5 / 512, scale=0.0) for a in range(P)]
    AB2 = op("s", [NB, KK], S.activation, T.ab2[:, :], T.kk[:, 0:384], AF.Abs, bias=T.nb[:, 2:3])
    AB1 = op("s", [], S.activation, T.ab1[:, :], T.kk[:, 0:256], AF.Abs, bias=T.nb[:, 1:2])
    AB0 = op("v", [NB, KK], V.tensor_scalar, T.ab0[:, :], T.kk[:, 0:128], T.nb[:, 0:1], None, A.add)
    EY = op("v", [EH0, EH1], V.tensor_tensor, T.ey[:, :], T.h0[:, :], T.h1[:, :], A.add)
    MK = op("v", [II, PF], V.tensor_scalar, T.mask[:, :], T.ii[:, 0:32], T.pf[:, 3:4], 0.5, A.subtract, A.is_lt)
    RR = [op("v", [AB0], V.tensor_reduce, T.rr[:, 0:1], T.ab0[:, :], X, A.min, apply_absolute_value=True)]
    EHO = op("v", [EY], V.tensor_copy, T.hoff[:, :], T.ey[:, :])
    RR += [op("v", [AB2], V.tensor_reduce, T.rr[:, 2:3], T.ab2[:, :], X, A.min),
           op("v", [AB1], V.tensor_reduce, T.rr[:, 1:2], T.ab1[:, :], X, A.min)]
    B1 = op("s", [EY, NQ], S.activation, T.b1[:, :], T.ey[:, :], AF.Abs, bias=T.nq[:, 0:1], scale=1.0 / 512)
    SGN = op("s", [B1], S.activation, T.sgn[:, :], T.b1[:, :], AF.Sign, bias=0.5, scale=-1.0)
    INR = op("s", [SGN], S.activation, T.inr[:, :], T.sgn[:, :], AF.Relu)

    def quarters(place, src, n, deps, give=()):
        out = []
        for d in range(P):
            for a in range(P):
                o_, i_ = place(d, a), src[32 * a:32 * a + 32, 0:n]
                if d % 2 == 0 and (d, a) not in give:
                    out.append(op("v", deps, V.tensor_copy, o_, i_))
                else:
                    out.append(op("s", deps, S.activation, o_, i_, AF.Copy))
        return out

    YY = quarters(lambda d, a: T.yy[32 * d:32 * d + 32, a:12:4], T.rr, 3, [RR])
    ZZ = op("s", [], S.activation, T.zero[:, :], T.ii[:, 0:12], AF.Copy, scale=0.0)
    O32 = op("s", [], S.activation, T.ones[:, :], T.ii[:, 0:32], AF.Identity, bias=1.0, scale=0.0)
    EV = op("s", [EHO, lk], S.activation, T.ev[:, :], T.lutk[:, 0:2560].indirect(T.hoff[:, 0:12]), AF.Copy)
    CW0 = op("s", [], S.activation, T.cw[:, 0:CAPP], T.ii[:, 0:CAPP], AF.Copy, scale=0.0)
    TT = op("v", [IDX, INR], V.tensor_tensor, T.tt[:, :], T.idx[:, :], T.inr[:, :], A.mult)
    IN = op("v", [YY, TT], V.tensor_tensor, T.ind[:, :], T.yy[:, :], T.tt[:, :], A.is_equal)
    NI = op("v", [], V.tensor_tensor, T.nind[:, :], T.yy[:, :], T.tt[:, :], A.not_equal)
    CC = op("v", [IN, ZZ], V.tensor_tensor_scan, T.cc[:, :], T.ind[:, :], T.zero[:, :], -1.0, A.add, A.add)
    P1 = op("v", [NI, TR], V.tensor_tensor, T.p1[:, :], T.nind[:, :], T.trash[:, :], A.mult)
    RP = op("v", [CC, O32], V.tensor_scalar, T.rp[:, :], T.ones[:, :], T.cc[:, 11:12], None, A.add)
    WW = op("v", [P1, CC], V.tensor_tensor, T.ww[:, :], T.cc[:, :], T.p1[:, :], A.add)
    RT = op("v", [RP], V.transpose, T.rt[:, :], T.rp[:, :])
    MM = op("v", [RT, MK], V.tensor_tensor, T.mm[:, :], T.rt[:, :], T.mask[:, :], A.mult)
    BS = op("v", [MM], V.tensor_reduce, T.base[:, :], T.mm[:, :], X, A.add)
    ZO = op("v", [WW, BS], V.tensor_scalar, T.zo[:, :], T.ww[:, :], T.base[:, 0:1], None, A.add)
    CR = op("v", [CR0, PF], V.tensor_scalar, T.cr[:, :], T.cr0[:, :], T.pf[:, 0:1], None, A.add)
    CW = op("v", [ZO, EV, CW0], V.tensor_copy, T.cw[:, 0:512].indirect(T.zo[:, 0:12]), T.ev[:, :])
    DD = op("v", [CW, CR], V.tensor_copy, T.dd[:, :], T.cw[:, 0:CAPP].indirect(T.cr[:, 0:8]))
    DT = op("v", [DD], V.transpose, T.dtr[:, :], T.dd[:, :])
    LQ = op("v", [DT], V.tensor_tensor, T.lq[:, :], T.dtr[:, 0:128:32], T.dtr[:, 16:128:32], A.add)
    LS = quarters(lambda d, a: T.ls[32 * d:32 * d + 32, 4 * a:4 * a + 4], T.lq, 4, [LQ])
    need("g", [LS])

    def send(items, local):
        tr = []
        for j, (a, src, dst, sem) in enumerate(items):
            c = T.cores[peers[a]]
            rid, pid, _ = topo.addr(c)
            es = topo.engines(core, c)
            n = len(es) // len(items)
            m = 0
            for e in es[j * n:j * n + n]:
                m |= 1 << e
            tr.append(RemoteDMATransfer(dst_ids=[DstId(rid=rid, pnc=pid)], dma_engine_mask=m, remote_sem=sem, src=src, dst=dst))
        g.remote_dma_fused(tr, local_sem=local)

    back = [(r - peers[a] - 1) % N for a in range(P)]
    ne = len(topo.engines(core, T.cores[peers[0]]))
    send([(a, T.ls[:, 4 * a:4 * a + 4], T.lin[:, 4 * back[a]:4 * back[a] + 4], T.sem.larr) for a in range(P)], T.sem.lloc)

    QW = op("v", [DWT], V.quantize_mx, T.qw[:, :], T.sw[:, :], T.ws[:, :])
    ZF0 = op("v", [], V.memset, T.zf[:, :], 0.0)
    FI = op("v", [YY], V.tensor_scalar, T.fi[:, :], T.yy[:, :], -1.0, None, A.add)
    ZF = [op("v", [ZF0, WW, BS], V.tensor_scalar, T.zf[:, c:c + 12], T.ww[:, :], T.base[:, 0:1], None, A.add) for c in (0, 16)]
    FA = op("v", [FI], V.tensor_scalar, T.fa[:, :], T.fi[:, :], 31, None, A.bitwise_and)
    ZT = op("v", [ZF], V.transpose, T.zt[:, :], T.zf[:, :])
    FB = op("v", [FI], V.tensor_scalar, T.fb[:, :], T.fi[:, :], 5, None, A.arith_shift_right)
    ZU = op("v", [ZT], V.tensor_copy, T.zu[:, :], T.zt[:, :])
    SF = op("s", [ZU, lk], S.activation, T.sf[:, :], T.lutk[:, 0:512].indirect(T.zu[:, 0:32]), AF.Copy)
    OC = op("v", [TP], V.tensor_scalar, T.oc[:, :], T.tabp[:, :], 4.0, float(-4 * TB * r), A.mult, A.add)
    FA6 = op("v", [FA], V.tensor_scalar, T.fa16[:, :], T.fa[:, :], 16.0, None, A.mult)
    OD = op("v", [OC], V.tensor_scalar, T.od[:, :], T.oc[:, :], 0.0, float(4 * TB - 4), A.max, A.min)
    FDF = op("v", [FA6, FB], V.tensor_tensor, T.fdf[:, :], T.fa16[:, :], T.fb[:, :], A.add)
    OO = [op("v", [OD], V.tensor_scalar, T.offo[:, 24 * t:24 * t + 24], T.od[:, :], float(t), None, A.add) for t in range(2)]
    FD = [op("v", [FDF], V.tensor_copy, T.fd[:, h:24:2], T.fdf[:, :]) for h in range(2)]

    def gather(t, out, offsets, deps):
        win = T.xs[:, 0:2046] if t < 2 else T.x2[:, 16:2062]
        if t < 2:
            return op("v", [deps[t % 2], DX], V.tensor_copy, out, win.indirect(offsets))
        return op("s", [deps[t % 2], DX], S.activation, out, win.indirect(offsets), AF.Copy)

    LA = ("larr", ne)
    OX = [op("v", [LA], V.tensor_scalar, T.offx[:, 16 * t:16 * t + 16], T.lin[:, :], 1.0 / 256, float(t - 4 * TB * r), A.mult, A.add)
          for t in range(2)]
    QX = []
    for h in range(2):
        HX = [gather(t, T.hx[:, 512 * h + t:512 * h + 512:4], T.offx[:, 16 * (t % 2) + 8 * h:16 * (t % 2) + 8 * h + 8], OX) for t in range(4)]
        c = slice(128 * h, 128 * h + 128)
        QX.append(op("v", [HX], V.quantize_mx, T.qx[:, c], T.sx[:, c], T.hx[:, 512 * h:512 * h + 512]))
        need("g", [QX])
        pair, sem = (2 * h, 2 * h + 1), T.sem["carr%d" % h]
        send([(a, T.qx[:, 64 * a:64 * a + 64].bitcast(dt.uint8), T.qr[:, 64 * back[a]:64 * back[a] + 64].bitcast(dt.uint8), sem)
              for a in pair], T.sem.cloc)
        send([(a, T.sx[:, 64 * a:64 * a + 64], T.sr[:, 64 * back[a]:64 * back[a] + 64], sem) for a in pair], T.sem.cloc)

    HO_ = [gather(t, T.ho[:, t:1536:4], T.offo[:, 24 * (t % 2):24 * (t % 2) + 24], OO) for t in range(4)]
    SG = op("s", [FD, SF], S.activation, T.sg[:, :], T.sf[:, 0:512].indirect(T.fd[:, 0:24]), AF.Copy)
    B1N = op("s", [NQ, TP], S.activation, T.b1n[:, :], T.tabp[:, :], AF.Abs, bias=T.nq[:, 0:1], scale=1.0 / 512)
    QO = op("v", [HO_], V.quantize_mx, T.qo[:, :], T.so[:, :], T.ho[:, :])

    def product(o, out, codes, plane, deps):
        return op("t", deps, M.matmul_mx, out, T.qw[:, 128 * o:128 * o + 128], T.sw[:, 128 * o:128 * o + 128], codes, plane, True, True)

    MO = [product(o, T.pso[:, 512 * o:512 * o + 384], T.qo[:, :], T.so[:, :], [QO, QW]) for o in range(O)]
    A64 = [op("v", [], V.memset, T.a64[32 * a:32 * a + 32, :], float(CAPP * a)) for a in range(P)]
    OI = op("v", [I16], V.tensor_scalar, T.oi[:, :], T.i16[:, :], T.pf[:, 0:1], float(CAPP * P), A.add, A.add)
    OE = op("v", [TP], V.tensor_scalar, T.oe[:, :], T.tabp[:, :], float(TB * r), None, A.is_ge)
    OA = op("v", [TP], V.tensor_scalar, T.oa[:, :], T.tabp[:, :], float(TB * r + TB), None, A.is_lt)
    SGT = op("v", [SG], V.transpose, T.sgt[:, :], T.sg[:, :])
    INN = op("v", [B1N], V.tensor_scalar, T.inrn[:, :], T.b1n[:, :], 0.5, None, A.is_lt)
    Q0 = [op("v", [SGT, A64], V.tensor_scalar, T.q0[:, h:24:2], T.sgt[:, 16 * h:384:32], 1.0 / 1024, T.a64[:, 0:1], A.mult, A.add)
          for h in range(2)]
    OM = op("v", [OE, OA], V.tensor_tensor, T.om[:, :], T.oe[:, :], T.oa[:, :], A.mult)
    Q1 = op("v", [Q0, INN], V.tensor_tensor, T.q1[:, :], T.q0[:, :], T.inrn[:, :], A.mult)
    QA = [op("v", [Q1], V.tensor_copy, T.qa[64 * h:64 * h + 64, :], T.q1[64 - 64 * h:128 - 64 * h, :]) for h in range(2)]
    Q2 = op("v", [QA, Q1], V.tensor_tensor, T.q2[:, :], T.q1[:, :], T.qa[:, :], A.add)
    QB = [op("v", [Q2], V.tensor_copy, T.qb[32 * a:32 * a + 32, :], T.q2[32 * (a ^ 1):32 * (a ^ 1) + 32, :]) for a in range(P)]
    OV = op("v", [OM, OI], V.tensor_tensor, T.ov[:, :], T.om[:, :], T.oi[:, :], A.mult)
    Q3 = op("v", [QB, Q2], V.tensor_tensor, T.q3[:, :], T.q2[:, :], T.qb[:, :], A.add)
    Q4 = op("v", [Q3, OV], V.tensor_tensor, T.q4[:, :], T.q3[:, :], T.ov[:, :], A.add)
    YO = op("v", [Q4], V.tensor_copy, T.yoff[:, :], T.q4[:, :])
    PO = [op("v", [MO[0]], V.tensor_copy, T.py0[:, 256:640], T.pso[:, 0:384]),
          op("s", [MO[1]], S.activation, T.py1[:, 256:640], T.pso[:, 512:896], AF.Copy)]

    PR = [[], []]
    for h in range(2):
        c = 64 * min(back[2 * h], back[2 * h + 1])
        for o in range(O):
            b = 512 * (2 * h + o)
            m = product(o, T.psr[:, b:b + 128], T.qr[:, c:c + 128], T.sr[:, c:c + 128], [("carr%d" % h, 2 * ne), QW])
            if o == 0:
                PR[0].append(op("v", [m], V.tensor_copy, T.py0[:, c:c + 128], T.psr[:, b:b + 128]))
            else:
                PR[1].append(op("s", [m], S.activation, T.py1[:, c:c + 128], T.psr[:, b:b + 128], AF.Copy))
    nd = 0
    for h in range(2):
        c = 192 * h
        Y0 = op("v", [PR[0], PO[0], YO], V.tensor_copy, T.yo[:, c:c + 192], T.py0[:, 0:640].indirect(T.yoff[:, 12 * h:12 * h + 12]))
        Y1 = op("s", [PR[1], PO[1], YO], S.activation, T.yo[:, 384 + c:384 + c + 192], T.py1[:, 0:640].indirect(T.yoff[:, 12 * h:12 * h + 12]), AF.Copy)
        for o, tok in ((0, Y0), (1, Y1)):
            need("y", [tok])
            g.sync.dma_start(T.y[:, 384 * o + c:384 * o + c + 192], T.yo[:, 384 * o + c:384 * o + c + 192]).then_inc(T.sem.dy, 16)
            nd += 16
    need("y", [("dy", nd)])
    need("g", [("lloc", ne), ("cloc", 4 * ne)] + [("c" + q, cnt[q]) for q in cnt])
